import numpy as np, ml_dtypes
CORES = [40,41,42,43,44,45,46,47]
N = 8
BF = ml_dtypes.bfloat16
V, C, T, S, VT, DR, DG = 3072, 192, 5, 16, 10, 3, 3
def start(s0, w0):
    H = np.full((N, 8, 16, C), -1, np.int64); H[:, :, 0] = s0; live = s0 >= 0
    return H, np.where(live[:, :, None], w0, np.float32(0)), live
def grow(t, H, W, live, nt, qt, u):
    nk = np.take_along_axis(nt, np.where(live, H[:, :, t], 0)[:, :, None, :], 3)
    shut = np.zeros(nk.shape, bool)
    for p in range(t + 1): shut |= nk == H[:, :, p:p + 1]
    x = np.take_along_axis(qt, nk.reshape(N, 8, 1, 16 * C), 3).reshape(N, 8, 16, 16, C)
    P = np.add.accumulate(np.where(shut[:, :, None], 0, x), axis=3); full = P[:, :, :, 15]
    votes = np.sum(256 * P > u[:, :, None, None, :] * full[:, :, :, None], axis=2)
    k = np.argmax((votes >= VT) & ~shut, axis=2); site = np.take_along_axis(nk, k[:, :, None, :], 2)[:, :, 0]
    moved = live & ~np.all(shut, axis=2)
    H = H.copy(); H[:, :, t + 1] = np.where(moved, site, -1)
    W = np.where(moved[:, :, None], W * full.astype(np.float32) * np.float32(2.0 ** -11), np.float32(0))
    return H, W, moved
def breed(H, W, live, old, lo, hi, coin):
    low = live & (np.sum(W < lo[..., None], axis=2) >= VT); high = live & (np.sum(W > hi[..., None], axis=2) >= VT)
    W = np.where(high[:, :, None], W * np.float32(0.5), np.where(low[:, :, None], W * np.float32(2), W))
    live = live & ~(low & (coin == 0)); H = H.copy()
    up = np.sum(high, axis=(0, 2)) > np.sum(old & ~live, axis=(0, 2))
    over, left = {}, {}
    for a in range(N):
        for g in range(8):
            src = np.flatnonzero(high[a, g]); hole = np.flatnonzero(~live[a, g]); n = min(len(src), len(hole))
            H[a, g][:, hole[:n]] = H[a, g][:, src[:n]]; W[a, g][:, hole[:n]] = W[a, g][:, src[:n]]; live[a, g, hole[:n]] = True
            over[a, g] = (H[a, g][:, src[n:n + S]], W[a, g][:, src[n:n + S]]); left[a, g] = hole[n:]
    for a in range(N):
        for g in range(8):
            h, w = over[(a - DR) % N, (g - DG) % 8]; hole = left[a, g][:h.shape[1]]; m = len(hole)
            H[a, g][:, hole] = h[:, :m]; W[a, g][:, hole] = w[:, :m]; live[a, g, hole] = True
    return H, W, live, up
def land(rng, traps):
    ring = np.argsort(rng.random((N, 8, V)), axis=-1); x = np.arange(V); sh = (N, 8, 16, V)
    to = np.where(rng.random(sh) < 0.4, (x + rng.integers(-6, 7, sh)) % V, rng.integers(0, V, sh))
    m = np.repeat(rng.integers(1, 5, (N, 8, V // 4)), 4, axis=-1)[:, :, None]; trap = np.repeat(rng.random((N, 8, V // 4)) < traps, 4, axis=-1)[:, :, None]
    to = np.where(trap, 4 * (x // 4) + (rng.random(sh) * m).astype(np.int64), to)
    return np.take_along_axis(np.take_along_axis(ring[:, :, None], to, 3), np.argsort(ring, axis=-1)[:, :, None], 3)
def base(rng, traps, dead):
    qt = np.clip(np.rint(rng.uniform(40, 200, (N, 8, 1, V)) * rng.uniform(0.6, 1.4, (N, 8, 16, V))), 16, 255).astype(np.int32)
    s0 = np.where(rng.random((N, 8, C)) < dead * rng.random((N, 8, 1)), -1, rng.integers(0, V, (N, 8, C)))
    w0 = np.exp2(rng.uniform(-2, 2, (N, 8, 1, C)) + rng.uniform(-1, 1, (N, 8, 16, 1)) + rng.uniform(-0.2, 0.2, (N, 8, 16, C))).astype(np.float32)
    return dict(nt=land(rng, traps), qt=qt, s0=s0, w0=w0, u=rng.integers(0, 256, (N, 8, T, C)), coin=rng.integers(0, 2, (N, 8, T, C)))
def limits(rng, W, live, na, nh, sharp):
    lo = np.ones((N, 8, 16), np.float32); hi = np.ones((N, 8, 16), np.float32); tiny = np.float32(0); huge = np.float32(2.0 ** 100)
    for a in range(N):
        for g in range(8):
            m = np.flatnonzero(live[a, g]); n = len(m)
            if n == 0: continue
            w = W[a, g][:, m]; o = np.argsort(np.add.reduce(np.log2(w), axis=0), kind="stable"); i = int(na[a, g]); j = n - 1 - int(nh[a, g])
            least = np.minimum.reduce(w, axis=1) * np.float32(0.5); most = np.maximum.reduce(w, axis=1) * np.float32(2)
            r1 = rng.permutation(16) < rng.choice(np.array([0, VT - 1, VT, 16])); r2 = rng.permutation(16) < rng.choice(np.array([0, VT - 1, VT, 16]))
            if i < 0: l = least
            elif i >= n: l = most
            elif sharp[a, g]: l = np.where(r1, np.nextafter(w[:, o[i]], huge), w[:, o[i]])
            else: l = w[:, o[i]] * np.float32(0.25)
            if j >= n: h = most
            elif j < 0: h = least
            elif sharp[a, g] == 2:
                v = np.sort(w, axis=0)[16 - VT]
                h = np.full(16, np.max(v[v < np.max(v)], initial=np.min(v) * np.float32(0.5)), np.float32)
            elif sharp[a, g]: h = np.where(r2, np.nextafter(w[:, o[j]], tiny), w[:, o[j]])
            else: h = w[:, o[j]] * np.float32(4)
            lo[a, g] = np.minimum(l, h); hi[a, g] = h
    return lo, hi
def tilt(rng, coin, W, live, old, lo, hi, tip):
    low = live & (np.sum(W < lo[..., None], axis=2) >= VT); high = live & (np.sum(W > hi[..., None], axis=2) >= VT)
    for g in tip:
        m = np.flatnonzero(low[:, g].reshape(-1)); k = int(np.sum(high[:, g])) - int(np.sum(old[:, g] & ~live[:, g])) - tip[g]
        z = coin[:, g].copy().reshape(-1); z[m] = 1; z[rng.permutation(m)[:max(k, 0)]] = 0
        coin[:, g] = z.reshape(N, C)
def finish(rng, d, goal):
    H, W, live = start(d["s0"], d["w0"]); f = np.ones(8, np.float32); lo = np.ones((N, 8, 16, T), np.float32); hi = np.ones((N, 8, 16, T), np.float32)
    for t in range(T):
        old = live
        H, W, live = grow(t, H, W, live, d["nt"], d["qt"], d["u"][:, :, t])
        aim = goal(t, np.sum(live, axis=2))
        l, h = limits(rng, W, live, aim[0], aim[1], aim[2])
        if len(aim) > 3: tilt(rng, d["coin"][:, :, t], W, live, old, l, h, aim[3])
        lo[..., t] = l * f[:, None]; hi[..., t] = h * f[:, None]
        H, W, live, up = breed(H, W, live, old, l, h, d["coin"][:, :, t])
        f = np.where(up, f * np.float32(0.5), f)
    return {"nb": np.ascontiguousarray(d["nt"].reshape(N, 128, V)).astype(np.int32), "qs": d["qt"].reshape(N, 128, V).astype(np.float32).astype(BF),
            "s0": d["s0"].astype(np.int32), "w0": np.ascontiguousarray(d["w0"].reshape(N, 128, C)).astype(np.float32),
            "us": np.ascontiguousarray(d["u"].reshape(N, 8, T * C)).astype(np.int32), "coin": np.ascontiguousarray(d["coin"].reshape(N, 8, T * C)).astype(np.int32),
            "lo": lo.reshape(N, 128, T), "hi": hi.reshape(N, 128, T)}
def sway(rng, n, k):
    up = (rng.permutation(8) < k)[None, :]
    a = np.where(up, rng.uniform(0.03, 0.12, (N, 8)), rng.uniform(0.3, 0.5, (N, 8))); b = np.where(up, rng.uniform(0.25, 0.45, (N, 8)), rng.uniform(0.03, 0.12, (N, 8)))
    return (a * n).astype(np.int64), (b * n).astype(np.int64), np.ones((N, 8), bool)
def setup_inputs(rng):
    return finish(rng, base(rng, 0.1, 0.3), lambda t, n: sway(rng, n, 4))
def setup_inputs_calm(rng):
    o = rng.permutation(8); num = np.zeros(8, np.int64); few = np.zeros(8, bool); num[o] = np.arange(8) % 4; few[o[:4]] = True
    d = base(rng, np.where(few, 0.0, 0.05)[:, None], 0.0)
    odd = (np.arange(N)[:, None] + np.arange(8)[None, :]) % 2 == 1
    d["qt"] = np.where(odd[:, :, None, None], rng.integers(60, 200, (N, 8, 16, 1)), d["qt"]).astype(np.int32)
    d["u"] = np.where(odd[:, :, None, None], 16 * rng.integers(0, 16, (N, 8, T, C)), d["u"])
    def goal(t, n):
        rich = (np.arange(N)[:, None] + t + num[None, :]) % 2 == 0; tip = {}
        a = np.where(few[None, :], 0.3, np.where(rich, 0.12, 0.5)) * rng.uniform(0.9, 1.0, (N, 8)); b = np.where(rich, 0.3, 0.05) * rng.uniform(0.9, 1.0, (N, 8))
        na = (a * n).astype(np.int64); nh = (b * n).astype(np.int64); sharp = np.ones((N, 8), np.int64)
        for g in range(8):
            k = int(num[g])
            if few[g]:
                c = 1 + t % 3 if t < k else (t + k) % 4
                q = rng.permutation(N)[:c]; nh[:, g] = -1; nh[q, g] = 1; sharp[q, g] = 2
                tip[g] = 1 if t < k else 0
            else: tip[g] = 1 + (t + g) % 3 if t < k else -((t + k) % 2)
        return na, nh, sharp, tip
    return finish(rng, d, goal)
def setup_inputs_corners(rng):
    d = base(rng, 0.0, 0.0); d["s0"] = rng.integers(0, V, (N, 8, C))
    d["w0"] = np.exp2(rng.uniform(-0.4, 0.4, (N, 8, 1, C)) + rng.uniform(-1, 1, (N, 8, 16, 1))).astype(np.float32)
    d["u"] = np.where(rng.random(d["u"].shape) < 0.3, 255 * rng.integers(0, 2, d["u"].shape), d["u"])
    cases = [(0, 0, S), (0, 0, C), (C, 0, 0), (C - 1, 0, 1), (40, 24, 64), (40, 24, 65 + S), (40, 24, 63 + S), (40, 24, 64 - S), (40, 24, 65 - S), (0, C, 0), (0, C - 1, 0), (0, 0, 0)]
    kind = rng.integers(0, 12, (N, 8)); o = rng.permutation(8)
    for a in range(N): kind[a, a % 8] = 5
    for i in range(8):
        kind[0, o[i]] = (0, 1, 5, 6, 0, 5, 1, 6)[i]; kind[DR % N, (o[i] + DG) % 8] = (7, 8, 7, 8, 2, 3, 4, 7)[i]
    na = np.zeros((N, 8), np.int64); nh = np.zeros((N, 8), np.int64)
    for a in range(N):
        for g in range(8):
            z, k, m = cases[kind[a, g]]; p = rng.permutation(C); na[a, g] = k; nh[a, g] = m
            d["s0"][a, g, p[:z]] = -1; d["coin"][a, g, 0, p[z:z + k]] = 0
            d["w0"][a, g][:, p[z:z + k]] *= np.float32(2.0 ** -6); d["w0"][a, g][:, p[z + k:z + k + m]] *= np.float32(64)
    return finish(rng, d, lambda t, n: (na, nh, np.zeros((N, 8), bool)) if t == 0 else sway(rng, n, 4))
def setup_inputs_crowd(rng):
    d = base(rng, 0.0, 0.0); kind = [list("ABDFGHIJ")[i] for i in rng.permutation(8)]; far = int(rng.integers(0, N))
    i = kind.index("A"); j = (kind.index("D") - DG) % 8; kind[i], kind[j] = kind[j], kind[i]
    fall = rng.permutation(N)[:(N // 2 if C > 255 else N - 2)].tolist()
    d["w0"] = np.exp2(rng.uniform(-0.4, 0.4, (N, 8, 1, C)) + rng.uniform(-1, 1, (N, 8, 16, 1))).astype(np.float32)
    na = np.full((N, 8), -1, np.int64); nh = np.full((N, 8), -1, np.int64); big = np.float32(64); small = np.float32(2.0 ** -6)
    for a in range(N):
        for g in range(8):
            c = kind[g]; one = (0, C - 1, int(rng.integers(0, C)))[int(rng.integers(0, 3))]; w = d["w0"][a, g]
            if c == "A":
                nh[a, g] = C
                if a % 2 == 0: d["s0"][a, g] = V - 1
            elif c == "B": nh[a, g] = C - 1; w[:, one] *= small
            elif (c == "H" and a % 2 == 0) or (c == "J" and a not in fall): nh[a, g] = C
            elif c == "D" or c == "J": d["coin"][a, g, 0] = 0; na[a, g] = C
            elif c == "H": d["coin"][a, g, 0] = 0; na[a, g] = C - 1; w[:, one] *= big
            elif c == "G":
                b = C // 4; p = rng.permutation(C); v = int(rng.integers(1, V - 1)); s = d["s0"][a, g]
                s[s == v] = 0; s[p[:b]] = v; d["nt"][a, g][:, v] = v
                na[a, g] = b; nh[a, g] = C - 2 * b; d["coin"][a, g, 0] = 0; w[:, p[b:2 * b]] *= small; w[:, p[2 * b:]] *= big
            else:
                k = C // 2; m = C - k; p = rng.permutation(C)
                if a == far and c == "F": k = k - 1
                if a == far and c == "I": m = m - 1
                na[a, g] = k; nh[a, g] = m
                d["coin"][a, g, 0] = 0; w[:, p[:k]] *= small; w[:, p[C - m:]] *= big
    def goal(t, n):
        if t == 0: return na, nh, np.zeros((N, 8), bool)
        a, b, s = sway(rng, n, 4)
        for g in range(8):
            if t < T - 1 and (kind[g] == "A" or kind[g] == "B"): a[:, g] = -1; b[:, g] = -1 if (kind[g] == "B" and t == 1) else C
        return a, b, s
    return finish(rng, d, goal)
def setup_inputs_ends(rng):
    d = base(rng, 0.0, 0.0); sh = (N, 8, 16, V)
    end = rng.random(sh) < np.where(rng.random((N, 8, 1, V)) < 0.3, 1.0, 0.55)
    d["nt"] = np.where(end, (V - 1) * rng.integers(0, 2, sh), d["nt"])
    bit = np.where(rng.random((N, 8, 1, V)) < 0.5, rng.integers(0, 2, (N, 8, 1, V)), rng.integers(0, 2, sh))
    d["qt"] = (16 + 239 * bit).astype(np.int32)
    d["w0"] = np.ascontiguousarray(np.broadcast_to(np.exp2(32.0 * rng.integers(0, 2, (N, 8, 1, C)) - 16), (N, 8, 16, C))).astype(np.float32)
    for a in range(N):
        for g in range(8):
            p = 1 + rng.permutation(V - 2)[:40]; nt = d["nt"][a, g]; qt = d["qt"][a, g]; m = (a + g) % 4
            nt[::2, p] = rng.integers(1, V - 1, (8, 40)); nt[:, 0] = p[17:33]; qt[:, p[17:32]] = 255; qt[:, p[32]] = rng.integers(144, 255, 16)
            d["w0"][a, g][:, [0, C - 1]] = np.float32(2.0 ** 16 if m % 2 == 0 else 2.0 ** -16)
            if m % 2 == 0:
                nt[:, V - 1] = p[:16]; qt[:, p[:16]] = 255
                if m == 0: nt[:, p[:16]] = p[17:33][:, None]; nt[:, p[17:33]] = p[:16][:, None]
            else:
                nt[:, V - 1] = V - 1; nt[15, V - 1] = p[16]; qt[:, p[16]] = 16; nt[:, p[16]] = p[:16]
                if m == 1:
                    way = [V - 1, int(p[16])] + p[33:32 + T].tolist()
                    for j in range(T):
                        nt[:, way[j]] = way[j]; nt[15 if j == 0 else int(rng.integers(0, 16)), way[j]] = way[j + 1]; qt[:, way[j + 1]] = 16
                    d["coin"][a, g][:, ::3] = 1; d["coin"][a, g][:, C - 1] = 1
    r = rng.random((N, 8, C)); d["s0"] = np.where(r < 0.2, -1, np.where(r < 0.55, V - 1, np.where(r < 0.75, 0, rng.integers(0, V, (N, 8, C))))); d["s0"][..., 0] = V - 1; d["s0"][..., 1] = 0; d["s0"][..., C - 1] = V - 1
    d["u"] = np.where(rng.random(d["u"].shape) < 0.85, 255 * rng.integers(0, 2, d["u"].shape), d["u"])
    return finish(rng, d, lambda t, n: sway(rng, n, 6))
def setup_inputs_spread(rng):
    d = base(rng, 0.08, 0.3)
    d["qt"] = np.clip(np.rint(np.exp2(4 + 4 * rng.random((N, 8, 1, V)) + rng.uniform(-1, 1, (N, 8, 16, V)))), 16, 255).astype(np.int32)
    d["u"] = (256 * rng.random((N, 8, T, C)) ** 3).astype(np.int64)
    d["w0"] = np.exp2(rng.uniform(-6, 6, (N, 8, 1, C)) + rng.uniform(-2, 2, (N, 8, 16, 1)) + rng.uniform(-0.3, 0.3, (N, 8, 16, C))).astype(np.float32)
    return finish(rng, d, lambda t, n: sway(rng, n, 4))
def check_inputs(d):
    bad = []
    for k, a, b in (("nb", 0, V - 1), ("qs", 16, 255), ("s0", -1, V - 1), ("us", 0, 255), ("coin", 0, 1), ("w0", 2.0 ** -16, 2.0 ** 16), ("lo", 2.0 ** -90, 2.0 ** 90), ("hi", 2.0 ** -90, 2.0 ** 90)):
        v = np.asarray(d[k]).astype(np.float64)
        if not (np.min(v) >= a and np.max(v) <= b): bad.append("range of " + k)
    v = np.asarray(d["qs"]).astype(np.float64)
    if not np.all(v == np.floor(v)): bad.append("qs not whole")
    if not np.all(np.asarray(d["lo"]) <= np.asarray(d["hi"])): bad.append("lo over hi")
    return bad
def reference(nb, qs, s0, w0, us, coin, lo, hi):
    nt = nb.reshape(N, 8, 16, V); qt = qs.astype(np.float32).astype(np.int32).reshape(N, 8, 16, V)
    u = us.astype(np.int64).reshape(N, 8, T, C); cn = coin.reshape(N, 8, T, C)
    l = lo.astype(np.float32).reshape(N, 8, 16, T); h = hi.astype(np.float32).reshape(N, 8, 16, T)
    H, W, live = start(s0.astype(np.int64), w0.astype(np.float32).reshape(N, 8, 16, C)); F = np.ones(8, np.float32)
    for t in range(T):
        old = live
        H, W, live = grow(t, H, W, live, nt, qt, u[:, :, t])
        H, W, live, up = breed(H, W, live, old, l[..., t] * F[:, None], h[..., t] * F[:, None], cn[:, :, t])
        F = np.where(up, F * np.float32(2), F)
    H = np.where(live[:, :, None], H, -1); W = np.where(live[:, :, None], W, np.float32(0))
    return {"yh": H.reshape(N, 128, C).astype(np.float32), "yw": W.reshape(N, 128, C).astype(np.float32)}

@@ -1,0 +1,601 @@
+from concourse.bass import DstId, RemoteDMATransfer
+from concourse.mybir import AluOpType, ActivationFunctionType
+
+NS, L, NV, ST, DR = 3072, 192, 208, 5, 3
+O, ZC = 16, 224
+IDR, TZ, HB, TW = 400, 784, 992, 1184
+NO = 255 * 128
+F32, F16, BF, I32, U16 = "float32", "float16", "bfloat16", "int32", "uint16"
+
+SCRATCH = {}
+
+
+def _sb(names, cols, dtype):
+    for n in names.split():
+        SCRATCH[n] = ("sbuf", [128, cols], dtype)
+
+
+_sb("nbs", NS, I32); _sb("qw", NS + 16, BF); _sb("xq dd", 3344, BF); _sb("d0", 3344, F16)
+_sb("s0i", L, I32); _sb("usi coi", 960, I32); _sb("s0h", L, F16); _sb("ush coh", 960, F16)
+_sb("w0s lv", L, F32); _sb("lor hir", 8, F32); _sb("lh0 lh1", 16, F32)
+_sb("ub", 16 + ST * NV, BF); _sb("nco", 960, BF)
+_sb("offq", NV, U16); _sb("nk16 h16 yy nkn", NV, F16); _sb("eqs", 5 * NV, F16); _sb("ge", NV, BF)
+_sb("wv0 wv1 wv2 wv3 wv4 wv5 w2 hw hf nkm", 240, F32); _sb("w1", 224, F32)
+_sb("snd", 160, F32); _sb("cnt dif", 32, BF)
+_sb("nt", NV, F32); _sb("ti", NV, I32); _sb("mm", 608, F16); _sb("sg", 384, BF)
+_sb("fl", 32, F16); _sb("rr ga gb qa qb", 32, F32); _sb("so go soff aoff", 16, U16); _sb("srcw0 srcw1", 16, U16)
+_sb("tb", TW, BF); _sb("idv onesb", L, BF); _sb("srcb", 240, BF)
+_sb("nka eqa", 80, F16); _sb("asc", 16, F32); _sb("sm", 32, F32); _sb("junk", 192, F32)
+_sb("wo ho", NV, F32)
+_sb("jq", 256, F32); _sb("dq onef bt bf lf uf t1 t2 t3 t4 ba", 128, F32); _sb("pi", 8, I32); _sb("g8i", 144, I32); _sb("w8i", 144, I32)
+_sb("col", 32, F32); _sb("dg", 16, F32); _sb("da", 128, F32); _sb("jd db dc ds ssc", 240, BF); _sb("wsc", NV, F32); _sb("addc", 8, F32); _sb("jm cw idw", 16, F32); _sb("d0c", 32, F32)
+_sb("b16 i16 i4k trih uph trio upo r0 r1 r2 r3 r4 g8", 128, F16); _sb("f16 w8", 144, F16); _sb("fb", 144, BF)
+_sb("i2b bid ih iq i125", 128, BF); _sb("rw", 256, BF)
+for _i in range(8):
+    SCRATCH["p%d" % _i] = ("psum", [128, 512], F32)
+
+SEMAPHORES = (["ev", "es", "et", "eg", "loc"] + ["aw%d" % i for i in range(5)] + ["af%d" % i for i in range(4)]
+              + ["dm%d" % i for i in range(12)])
+
+CH0 = [(0, 64), (64, 128), (128, 192)]
+CH1 = [(0, 64), (64, 128), (128, 208)]
+GA0 = [("v", 0, 32), ("s", 32, 64), ("s", 64, 128), ("s", 128, 192)]
+GA1 = [("v", 0, 32), ("s", 32, 64), ("s", 64, 128), ("s", 128, 192), ("v", 192, 208)]
+GA4 = [("v", 0, 64), ("s", 64, 128), ("s", 128, 192), ("v", 192, 208)]
+CY, PC, HOP = 0.00104, 0.0006, 0.10
+LINK = 2.5
+ROUNDS, TEMP, SEED = 20000, 0.2, 1
+
+
+def build(g, core, T, topo):
+    rank = T.rank_of(core)
+    n_r = len(T.cores)
+    A = AluOpType
+    AF = ActivationFunctionType
+    nodes = []
+    acc = {}
+
+    def a(name, lo=0, hi=None, step=1, p=128):
+        if hi is None:
+            hi = SCRATCH[name][1][1]
+        v = T[name][0:p, lo:hi] if step == 1 else T[name][0:p, lo:hi:step]
+        return {"ap": v, "r": [(name, lo, hi)], "n": len(range(lo, hi, step)), "m": SCRATCH[name][0], "d": SCRATCH[name][2], "ind": 0}
+
+    def ind(win, off):
+        return {"ap": win["ap"].indirect(off["ap"]), "r": win["r"], "o": off["r"], "n": 16 * off["n"], "m": "sbuf", "d": win["d"], "ind": 1}
+
+    def node(eng, fn, outs, ins, cost, extra=(), lat=0.0, kind="c", sem=None, cnt=0):
+        k = len(nodes)
+        deps = set(extra)
+        wr = []; rd = []
+        for x in outs:
+            wr += x["r"]; rd += x.get("o", [])
+        for x in ins:
+            if isinstance(x, dict):
+                rd += x["r"] + x.get("o", [])
+        for regs, w in ((wr, True), (rd, False)):
+            for (nm, lo, hi) in regs:
+                ps = SCRATCH[nm][0] == "psum"
+                for (j, e2, l2, h2, w2) in acc.setdefault(nm, []):
+                    if j != k and (((w or w2) and lo < h2 and l2 < hi) or (ps and e2 != eng)):
+                        deps.add(j)
+                if w and not ps:
+                    acc[nm] = [z for z in acc[nm] if not (lo <= z[2] and z[3] <= hi)]
+                acc[nm].append((k, eng, lo, hi, w))
+        nodes.append({"e": eng, "f": fn, "deps": sorted(deps), "c": cost, "lat": lat, "k": kind, "sem": sem, "cnt": cnt, "nm": (wr[:1], rd[:2])})
+        return k
+
+    def P(x):
+        return x["ap"] if isinstance(x, dict) else x
+
+    def vc(out, ins, two=False):
+        xs = [out] + [x for x in ins if isinstance(x, dict) and x["n"] > 1]
+        n = max(x["n"] for x in xs)
+        if out["ind"]:
+            return 0.05 + n * 3.8 * CY
+        if any(x["ind"] for x in xs):
+            return 0.05 + n * 1.56 * CY
+        c = 0.5 if all(x["d"] in (F16, BF, U16) for x in xs) else 1.0
+        if two:
+            c = 2.0 if all(x["m"] == "sbuf" for x in ins) else 1.0
+        return 0.05 + max(64, n * c) * CY
+
+    def ts(out, i0, s1, s2, op0, op1=None, extra=()):
+        if op1 is None:
+            f = lambda: g.vector.tensor_scalar(P(out), P(i0), P(s1), None, op0)
+        else:
+            f = lambda: g.vector.tensor_scalar(P(out), P(i0), P(s1), P(s2), op0, op1)
+        return node("v", f, [out], [i0, s1, s2], vc(out, [i0]), extra)
+
+    def tt(out, i0, i1, op, extra=()):
+        return node("v", lambda: g.vector.tensor_tensor(P(out), P(i0), P(i1), op), [out], [i0, i1], vc(out, [i0, i1], True), extra)
+
+    def cp(out, i0, extra=()):
+        return node("v", lambda: g.vector.tensor_copy(P(out), P(i0)), [out], [i0], vc(out, [i0]), extra)
+
+    def ms(out, c):
+        return node("v", lambda: g.vector.memset(P(out), c), [out], [], vc(out, []))
+
+    def scan(out, d0, d1, init, op0, op1):
+        return node("v", lambda: g.vector.tensor_tensor_scan(P(out), P(d0), P(d1), init, op0, op1), [out], [d0, d1], vc(out, [d0, d1]))
+
+    def act(out, i0, func=None, bias=0.0, scale=1.0, accum=None, extra=()):
+        func = AF.Identity if func is None else func
+        n = max(out["n"], i0["n"])
+        cost = 0.07 + (n * 1.56 if i0["ind"] else max(64, n)) * CY
+        if accum is None:
+            f = lambda: g.scalar.activation(P(out), P(i0), func, bias=P(bias), scale=P(scale))
+            return node("s", f, [out], [i0, bias, scale], cost, extra)
+        f = lambda: g.scalar.activation(P(out), P(i0), func, bias=P(bias), scale=P(scale), accum_out=P(accum))
+        return node("s", f, [out, accum], [i0, bias, scale], cost + 0.02, extra)
+
+    def mm(out, pairs, extra=()):
+        def f():
+            r = None
+            for i, (l, x) in enumerate(pairs):
+                r = g.tensor.matmul(P(out), P(l), P(x), i == 0, i == len(pairs) - 1)
+            return r
+        ins = [z for pr in pairs for z in pr]
+        return node("t", f, [out], ins, 0.05 + len(pairs) * (max(64, out["n"]) * PC + 0.005), extra)
+
+    def iota(out, pat, base, cm):
+        if out["d"] == I32:
+            f = lambda: g.iota(P(out), pat, base, cm)
+        else:
+            f = lambda: g.iota(P(out), pat, base, cm, allow_small_or_imprecise_dtypes=True)
+        return node("g", f, [out], [], 0.13 + 2 * out["n"] * CY)
+
+    def asel(out, i0, pat, op, fill, base, cm):
+        return node("g", lambda: g.affine_select(P(out), P(i0), pat, op, fill, base, cm), [out], [i0], 0.17 + 2 * out["n"] * CY)
+
+    ndma = [0]
+
+    def dma(q, pairs, outs, ins, lat):
+        sem = "dm%d" % ndma[0]; ndma[0] += 1
+        eng = g.sync if q == "y" else g.scalar
+
+        def f():
+            for o_, i_ in pairs:
+                eng.dma_start(o_, i_).then_inc(T.sem[sem], 16)
+        return node(q, f, outs, ins, 0.06 * len(pairs), lat=lat, kind="d", sem=sem, cnt=16 * len(pairs))
+
+    sh = 16 * rank
+
+    def rot_in(name, src, lo, hi):
+        if sh == 0:
+            return [(T[name][:, lo:hi], src[:, :])]
+        return [(T[name][0:128 - sh, lo:hi], src[sh:128, :]), (T[name][128 - sh:128, lo:hi], src[0:sh, :])]
+
+    def rot_out(dst, name, lo, hi):
+        if sh == 0:
+            return [(dst[:, :], T[name][:, lo:hi])]
+        return [(dst[sh:128, :], T[name][0:128 - sh, lo:hi]), (dst[0:sh, :], T[name][128 - sh:128, lo:hi])]
+
+    dma("s", [(T.s0i[0:8, :], T.s0[:, :])], [a("s0i")], [], 2.0)
+    dma("y", rot_in("nbs", T.nb, 0, NS), [a("nbs")], [], 6.5)
+    dma("y", rot_in("qw", T.qs, 0, NS), [a("qw", 0, NS)], [], 9.0)
+    dma("s", rot_in("w0s", T.w0, 0, L), [a("w0s")], [], 3.0)
+    dma("s", [(T.usi[0:8, :], T.us[:, :]), (T.coi[0:8, :], T.coin[:, :])], [a("usi"), a("coi")], [], 3.0)
+    dma("s", rot_in("lor", T.lo, 0, ST) + rot_in("hir", T.hi, 0, ST), [a("lor"), a("hir")], [], 4.0)
+
+    c = lambda j: a("col", j, j + 1)
+    PM, P16, E15, TC, SC, THR, RM, RB, NTZ, AD, AD2, PM1, C200 = range(13)
+    iota(a("g8i", 0, 128, p=8), [[1, 8], [0, 16]], rank + 8, -1)
+    iota(a("w8i", p=8), [[1, 144]], 16 * rank + 240, -16)
+    iota(a("pi", 0, 1), [[0, 1]], 0, 1)
+    iota(a("jq"), [[1, 256]], 0, 0)
+    iota(a("dq"), [[1, 128]], 0, -1)
+    iota(a("jm"), [[16, 16]], 0, 0)
+    ts(a("g8i", 0, 128, p=8), a("g8i", 0, 128, p=8), 7, None, A.bitwise_and)
+    ts(a("g8", p=8), a("g8i", 0, 128, p=8), 0.0, None, A.is_equal)
+    ts(a("w8i", p=8), a("w8i", p=8), 127, None, A.bitwise_and)
+    ts(a("w8", p=8), a("w8i", p=8), 0.0, None, A.is_equal)
+    ts(a("pi", 1, 2), a("pi", 0, 1), 15, None, A.bitwise_and)
+    cp(c(PM), a("pi", 1, 2))
+    ts(c(P16), a("pi", 0, 1), c(PM), None, A.subtract)
+    ts(c(E15), c(PM), 15.0, None, A.is_equal)
+    act(c(TC), c(E15), scale=-16.0, bias=1.0)
+    act(c(SC), c(E15), bias=-0.5)
+    act(c(THR), c(E15), scale=16.0 * NO + 1280.0, bias=-16.0 * NO - 1216.0)
+    ts(c(RM), c(PM), 5.5, None, A.is_lt)
+    act(c(RB), c(RM), scale=1025.0, bias=-1.0)
+    act(c(NTZ), c(PM), scale=-1.0, bias=float(-TZ))
+    act(c(AD), c(E15), scale=-8192.0, bias=9216.0)
+    act(c(AD2), c(E15), scale=-256.0, bias=256.0)
+    act(c(PM1), c(PM), bias=1.0)
+    act(c(C200), c(PM), bias=200.0)
+    ms(a("onef"), 1.0)
+    asel(a("bt"), a("onef"), [[16, 8], [0, 16]], A.is_ge, 0.0, 15, -1)
+    asel(a("bf"), a("bt"), [[-16, 8], [0, 16]], A.is_ge, 0.0, 0, 1)
+    asel(a("lf"), a("bf"), [[1, 128]], A.is_ge, 0.0, 0, -1)
+    asel(a("uf"), a("bf"), [[-1, 128]], A.is_gt, 0.0, 0, 1)
+    for tmp, src, fill, dst in (("t1", "lf", TZ, "trih"), ("t2", "uf", 1 - TZ, "uph"), ("t3", "lf", HB, "trio"), ("t4", "uf", 1 - HB, "upo")):
+        asel(a(tmp), a(src), [[1, 128]], A.not_equal, float(fill), 0, -1)
+        cp(a(dst), a(tmp))
+    def fill(name, lo, hi, v):
+        for x in range(lo, hi, 256):
+            act(a(name, x, min(hi, x + 256)), a("jq", 0, min(hi, x + 256) - x), bias=v, scale=0.0)
+    cp(a("b16"), a("bf"))
+    ts(a("f16"), a("jq", 0, 144), c(P16), 16.0, A.subtract, A.is_equal)
+    ts(a("fb"), a("jq", 0, 144), c(P16), 16.0, A.subtract, A.is_equal)
+    for nm, v in (("i16", 1.0), ("i4k", 4096.0)):
+        ts(a(nm), a("dq"), 0.0, v, A.is_equal, A.mult)
+    ts(a("rw", 0, 128), a("dq"), 0.0, None, A.is_equal)
+    act(a("rw", 128, 256), a("rw", 0, 128))
+    for nm, v in (("i2b", 2.0 ** -6), ("ih", 0.5), ("iq", -0.25), ("i125", 1.25)):
+        act(a(nm), a("rw", 0, 128), scale=v)
+    ts(a("ba"), a("dq"), c(TC), c(SC), A.is_equal, A.mult)
+    tt(a("bid"), a("ba"), a("ih"), A.add)
+    ts(a("dg"), a("jq", 0, 16), c(PM), None, A.is_equal)
+    for p in range(5):
+        ts(a("r%d" % p), a("b16"), a("dg", p, p + 1), None, A.mult)
+    iota(a("jd"), [[0, 15], [1, 16]], 0, 0)
+    ts(a("db"), a("jd"), c(PM1), -256.0, A.is_equal, A.mult)
+    ts(a("dc"), a("jd"), c(PM), 2048.0, A.is_equal, A.mult)
+    tt(a("ds"), a("dc"), a("db"), A.add)
+    act(a("da"), a("ds", 0, 128), scale=32.0)
+    act(a("addc"), a("onef", 0, 8), scale=c(AD))
+    act(a("cw"), a("jm"), bias=c(C200))
+    act(a("idw"), a("cw"), bias=float(IDR - 200))
+    ts(a("go", 13, 15), a("onef", 0, 2), c(PM), float(HB - 1), A.add, A.add)
+    fill("tb", 0, IDR, 0.0); fill("tb", IDR + L, TW, float(ZC))
+    act(a("tb", IDR, IDR + L), a("jq", 0, L), bias=float(O))
+    act(a("idv"), a("jq", 0, L), bias=float(O))
+    fill("onesb", 0, L, 1.0)
+    fill("d0c", 0, 13, 1.0); fill("d0c", 13, 14, 0.0); fill("d0c", 14, 26, 1.0)
+    ms(a("fl", 0, 1), 0.0)
+    ms(a("mm", 192, 208), 0.0); ms(a("mm", 400, 416), 1.0)
+    for x in range(0, 3344, 836):
+        ms(a("d0", x, x + 836), 60000.0)
+    fill("xq", 0, 16, float(NO))
+    fill("qw", NS, NS + 16, 0.0)
+    fill("ub", 0, O, 0.0); fill("ub", NV, NV + O, 0.0)
+    fill("w1", 0, O, 0.0); fill("w2", 0, 240, 0.0); fill("hw", 0, 240, 0.0); fill("hf", 0, 240, -1.0); fill("nkm", 0, 240, 2048.0)
+    fill("wo", 0, O, 0.0); fill("ho", 0, O, 0.0)
+    E = lambda k: a("f16", 16 - k, 144 - k)
+    EB = lambda k: a("fb", 16 - k, 144 - k)
+
+    ts(a("ush", p=8), a("usi", p=8), -8.0, None, A.mult)
+    ts(a("coh", p=8), a("coi", p=8), -1.0, 1.0, A.mult, A.add)
+    for t in range(ST):
+        pb = "p%d" % (t % 2)
+        mm(a(pb, 0, L), [(a("g8", p=8), a("ush", t * L, t * L + L, p=8))])
+        mm(a(pb, L, 2 * L), [(a("g8", p=8), a("coh", t * L, t * L + L, p=8))])
+        act(a("ub", O + t * NV, O + t * NV + L), a(pb, 0, L))
+        act(a("nco", t * L, t * L + L), a(pb, L, 2 * L))
+    act(a("lh0", 0, ST), a("lor", 0, ST)); act(a("lh0", 8, 8 + ST), a("hir", 0, ST))
+    fill("lh0", 5, 8, 0.0); fill("lh0", 13, 16, 0.0)
+
+    ts(a("s0h", p=8), a("s0i", p=8), -1024.0, None, A.add)
+    mm(a("p6", 0, 12), [(a("w8", 16 - r, 144 - r, p=8), a("s0h", r, L, 16, p=8)) for r in range(16)])
+    ts(a("soff", 0, 12), a("p6", 0, 12), 1024.0, None, A.add)
+    mm(a("p3", 0, L), [(a("g8", p=8), a("s0h", p=8))])
+    mm(a("p4", 0, L), [(a("w8", 16, 144, p=8), a("s0h", p=8))])
+    ts(a("nkn", 0, L), ind(a("nbs"), a("soff", 0, 12)), -1024.0, None, A.add)
+    tt(a("eqs", 0, L), a("nkn", 0, L), a("p3", 0, L), A.is_equal)
+    mm(a("p7", 0, L), [(a("i16"), a("nkn", 0, L)), (a("i4k"), a("eqs", 0, L))])
+    ts(a("offq", 0, L), a("p7", 0, L), 1024.0, 3072.0, A.add, A.min)
+    cp(a("h16", 0, L), a("p4", 0, L))
+    ts(a("lv"), a("p3", 0, L), -1024.5, None, A.is_gt)
+    tt(a("wv0", 0, L), a("w0s"), a("lv"), A.mult)
+    s = lambda j: a("sm", j, j + 1)
+    PD, YY, NVA, SG, FA = range(5)
+    act(a("junk"), a("lv"), accum=s(NVA))
+    act(s(PD), s(NVA), bias=float(L), scale=-1.0)
+
+    peers = [T.cores[(rank + d) % n_r] for d in range(1, n_r)]
+    nxt = T.cores[(rank + DR) % n_r]
+    nloc = [0]
+    arr_w = None; arr_f = None
+    lh = "lh0"
+    for t in range(ST):
+        nv = L if t == 0 else NV
+        last = t == ST - 1
+        wv = "wv%d" % t
+        uo = O + t * NV
+        hw = "hf" if last else "hw"
+        if t > 0:
+            k = t + 1
+            cp(a("h16", L, NV), a(wv, NV, 224), extra=[arr_w])
+            for p in range(k):
+                mm(a("p7", 256 + 16 * p, 272 + 16 * p), [(a("r%d" % p), a("h16", L, NV))])
+            scan(a("asc"), a("da", 0, 16), a("p7", 256 + 16 * t, 272 + 16 * t), 0.0, A.add, A.min)
+            ts(a("aoff", 0, k), a("addc", 0, k), a("asc", 15, 16), 3071.0, A.add, A.min)
+            ts(a("nka", 0, 16 * k), ind(a("nbs"), a("aoff", 0, k)), -1024.0, None, A.add)
+            tt(a("eqa", 0, 16 * k), a("nka", 0, 16 * k), a("p7", 256, 256 + 16 * k), A.is_equal)
+            mm(a("p7", 352, 368), [(a("i16"), a("nka", 0, 16))] + [(a("i4k"), a("eqa", 16 * p, 16 * p + 16)) for p in range(k)])
+            ts(a("offq", L, NV), a("p7", 352, 368), 1024.0, 3072.0, A.add, A.min)
+            act(a("junk", 0, 16), a(wv, L, NV), AF.Sign, accum=s(NVA), extra=[arr_w])
+            act(s(PD), s(NVA), AF.Relu, bias=s(YY), scale=-1.0)
+            prs = [(a("rw", 0, 128), a("dif", 8 * t - 8, 8 * t - 7))]
+            for d in range(1, n_r):
+                r2 = 8 * t - 8 + (rank + d) % n_r
+                prs.append((a("rw", 128 - 16 * d, 256 - 16 * d), a("cnt", r2, r2 + 1)))
+            mm(a("p5", 300, 301), prs, extra=[arr_f])
+            act(s(SG), a("p5", 300, 301), AF.Sign, bias=-0.5)
+            act(s(FA), s(SG), bias=1.5, scale=0.5)
+            lh2 = "lh%d" % (t % 2)
+            act(a(lh2), a(lh), scale=s(FA))
+            lh = lh2
+        ts(a("nk16", 0, 128), a("offq", 0, 128), -1024.0, None, A.add)
+        ts(a("nk16", 128, nv), a("offq", 128, nv), -1024.0, None, A.add)
+        act(a("p5", 0, L), a("nco", t * L, t * L + L), bias=2.0 ** -120, scale=a(lh, t, t + 1))
+        iota(a("tb", HB, HB + 16), [[1, 16]], 0, 0)
+        if not last:
+            for p in range(t + 1):
+                mm(a("p%d" % (3 + p // 2), NV * (p % 2), NV * (p % 2) + nv), [(a("r%d" % p), a("h16", 0, nv))])
+        prev = []
+        for (e, lo, hi) in (GA0 if t == 0 else GA4 if last else GA1):
+            src = ind(a("qw"), a("offq", lo, hi))
+            if e == "v":
+                ts(a("xq", 16 * lo + 16, 16 * hi + 16), src, 2.0 ** -5, None, A.mult)
+            else:
+                prev = [act(a("xq", 16 * lo + 16, 16 * hi + 16), src, scale=2.0 ** -5, extra=prev)]
+        prev = []
+        for ci, (lo, hi) in enumerate(CH0 if t == 0 else CH1):
+            n = hi - lo
+            bank = "p%d" % ci
+            pb = a(bank, 0, n)
+            x0, x1 = 16 * lo + 16, 16 * hi + 16
+            mm(pb, [(a("i2b"), a("xq", x0 + k, x1, 16)) for k in range(16)])
+            iota(a("xq", x0 + 15, x1, 16), [[0, hi - lo]], NO, 0)
+            tt(a("nt", lo, hi), pb, a("ub", uo + lo, uo + hi), A.mult)
+            tt(a("w1", O + lo, O + hi), pb, a(wv, lo, hi), A.mult, extra=[arr_w] if hi > L else [])
+            ts(a("ti", lo, hi), a("nt", lo, hi), 2047.0 + 255.0 / 512.0, None, A.add)
+            ts(a("d0", x0 - 1, x1 - 1, 16), a("ti", lo, hi), 2.0 ** -5, None, A.mult)
+            scan(a("dd", x0 - 1, x1 - 1), a("d0", x0 - 1, x1 - 1), a("xq", x0 - 1, x1 - 1), 60000.0, A.min, A.add)
+            mm(a(bank, 128, 128 + n), [(EB(k), a("dd", x0 + k, x1 - 1, 16)) for k in range(15)])
+            act(a("ge", lo, hi), a(bank, 128, 128 + n), AF.Sign, bias=c(THR))
+            mm(pb, [(a("bid"), a("ge", lo, hi))])
+            yy = a("yy", lo, hi)
+            tt(yy, pb, a("nk16", lo, hi), A.mult)
+            if not last:
+                mm(a(bank, 256, 256 + n), [(a("b16"), yy)])
+            hn = mm(a(bank, 384, 384 + n), [(a("i16"), a("h16", lo, hi)), (E(t + 1), yy)])
+            if last:
+                act(a(hw, O + lo, O + hi), a(bank, 384, 384 + n), bias=c(RB), scale=c(RM))
+                continue
+            act(a(hw, O + lo, O + hi), a(bank, 384, 384 + n))
+            scan(a("wsc", lo, hi), a("da", 0, n), a(bank, 256, 256 + n), 0.0, A.add, A.min)
+            ts(a("soff", lo // 16, hi // 16), a("wsc", lo + 15, hi, 16), c(AD), 3071.0, A.add, A.min)
+            nk = a("nkn", lo, hi)
+            ts(nk, ind(a("nbs"), a("soff", lo // 16, hi // 16)), -1024.0, None, A.add)
+            terms = [(a("i16"), nk)]
+            for p in range(t + 2):
+                hb = a(bank, 256, 256 + n) if p == t + 1 else a("p%d" % (3 + p // 2), NV * (p % 2) + lo, NV * (p % 2) + hi)
+                tt(a("eqs", NV * p + lo, NV * p + hi), nk, hb, A.is_equal)
+                terms.append((a("i4k"), a("eqs", NV * p + lo, NV * p + hi)))
+            mm(a(bank, 128, 128 + n), terms)
+            act(a("nkm", O + lo, O + hi), a(bank, 128, 128 + n))
+        dst = a("srcw%d" % ((t + 1) % 2), 14, 15)
+        if t > 0:
+            cp(ind(a("w1", 0, NV), dst), a("w1", NV, NV + 16))
+        w1 = a("w1", O, O + L)
+        ts(a("mm", 0, L), w1, a(lh, 8 + t, 9 + t), None, A.is_gt)
+        tt(a("mm", NV, NV + L), w1, a("p5", 0, L), A.is_lt)
+        ts(a("mm", 416, 608), w1, a(lh, t, t + 1), None, A.is_lt)
+        mm(a("p5", 200, 226), [(E(r), a("mm", r, 416, 16)) for r in range(16)])
+        ts(a("fl", 1, 27), a("p5", 200, 226), 9.5, None, A.is_gt)
+        mm(a("p5", 230, 243), [(a("trih"), a("fl", 1, 14)), (a("uph"), a("fl", 0, 13))])
+        mm(a("p5", 243, 256), [(a("trio"), a("fl", 14, 27)), (a("upo"), a("fl", 13, 26))])
+        scan(a("rr", 0, 26), a("d0c", 0, 26), a("p5", 230, 256), 0.0, A.mult, A.add)
+        nc = a("rr", 12, 13)
+        tt(a("qa", 0, 12), a("rr", 13, 25), a("cw", 0, 12), A.max)
+        tt(a("qb", 0, 12), a("qa", 0, 12), a("rr", 0, 12), A.max)
+        ts(a("so", 0, 12), a("qb", 0, 12), nc, None, A.subtract)
+        ts(a("ga", 0, 13), a("rr", 13, 26), nc, float(TZ - HB), A.subtract, A.add)
+        tt(a("gb", 0, 13), a("ga", 0, 13), a("idw", 0, 13), A.max)
+        ts(a("go", 0, 13), a("gb", 0, 13), float(TZ), None, A.min)
+        cp(ind(a("tb"), a("so", 0, 12)), a("idv"))
+        act(a("srcb"), ind(a("tb"), a("go", 0, 15)))
+        mm(a("p6", 0, L), [(a("b16"), a("mm", 0, L))])
+        mm(a("p6", L, 2 * L), [(a("b16"), a("mm", 416, 608))])
+        act(a("sg"), a("p6", 0, 2 * L), AF.Sign, bias=-9.5)
+        mm(a("p7", 0, L), [(a("iq"), a("sg", 0, L)), (a("ih"), a("sg", L, 2 * L)), (a("i125"), a("onesb"))])
+        tt(a("w2", O, O + L), w1, a("p7", 0, L), A.mult)
+        if t > 0:
+            if not last:
+                cp(ind(a("nkm", 0, NV), dst), a("nkm", NV, NV + 16))
+            cp(ind(a(hw, 0, NV), dst), a(hw, NV, NV + 16))
+        scan(a("ssc"), a("ds"), a("srcb"), 0.0, A.add, A.min)
+        sw = "srcw%d" % (t % 2)
+        ts(a(sw, 0, 15), a("ssc", 15, 240, 16), c(AD2), None, A.add)
+        src = a(sw, 0, 12); sur = a(sw, 12, 13); dst = a(sw, 14, 15)
+        so_ = 32 * t; wn = "wv%d" % (t + 1)
+        if not last:
+            ts(a("offq", 0, L), ind(a("nkm"), src), 1024.0, 3072.0, A.add, A.min)
+        act(a("snd", so_, so_ + 16), ind(a("w2"), sur))
+        act(a("snd", so_ + 16, so_ + 32), ind(a(hw), sur))
+        rid, pid, _ = topo.addr(nxt)
+        en = topo.engines(core, nxt)
+        ne = len(en) // 2
+        msk = sum(1 << x for x in en[:ne])
+
+        def send(so_=so_, wn=wn, t=t, rid=rid, pid=pid, msk=msk):
+            g.remote_dma(T[wn][:, L:224], T.snd[:, so_:so_ + 32], T.sem["aw%d" % t], T.sem.loc, pid, rid, msk)
+        sn = node("g", send, [], [a("snd", so_, so_ + 32)], 0.3, kind="r")
+        nloc[0] += ne
+        arr_w = node("x", None, [], [], 0.0, extra=[sn], lat=LINK, kind="a", sem="aw%d" % t, cnt=ne)
+        if last:
+            cp(a("wo", O, NV), ind(a("w2"), src))
+            act(a("ho", O, NV), ind(a(hw), src))
+            cp(ind(a("wo"), dst), a(wn, L, NV), extra=[arr_w])
+            cp(ind(a("ho"), dst), a(wn, NV, 224), extra=[arr_w])
+            dma("y", rot_out(T.yw, "wo", O, NV), [], [a("wo")], 2.0)
+            dma("s", rot_out(T.yh, "ho", O, NV), [], [a("ho")], 2.0)
+        else:
+            act(a(wn, 0, L), ind(a("w2"), src))
+            cp(a("h16", 0, L), ind(a(hw), src))
+            uo2 = uo + NV
+            act(a("ub", uo2 + L, uo2 + NV), ind(a("ub", uo2 - O, uo2 + L), dst))
+            act(s(YY), a("ga", 12, 13), bias=c(NTZ))
+            dif = a("dif", 8 * t, 8 * t + 1)
+            act(dif, s(YY), bias=s(PD), scale=-1.0)
+            m7 = sum(1 << x for x in en[ne:])
+            for q in peers:
+                m7 = m7 & topo.mask(core, q)
+            n7 = bin(m7).count("1")
+
+            def sendf(dif=dif, t=t, m7=m7):
+                ids = [DstId(rid=topo.addr(q)[0], pnc=topo.addr(q)[1]) for q in peers]
+                tr = RemoteDMATransfer(dst_ids=ids, dma_engine_mask=m7, remote_sem=T.sem["af%d" % t], srcs=[dif["ap"]],
+                                       dsts=[T.cnt[:, 8 * t + rank:8 * t + rank + 1] for q in peers])
+                g.remote_dma_fused([tr], local_sem=T.sem.loc)
+            sf = node("g", sendf, [], [dif], 0.5, kind="r")
+            nloc[0] += n7
+            arr_f = node("x", None, [], [], 0.0, extra=[sf], lat=LINK + 4.5, kind="a", sem="af%d" % t, cnt=n7 * (n_r - 1))
+    return nodes, nloc[0]
+
+
+def schedule(nodes):
+    n = len(nodes)
+    anc = [0] * n
+    pred = []
+    for k in range(n):
+        cover = 0
+        for d in nodes[k]["deps"]:
+            cover |= anc[d]
+        pred.append([d for d in nodes[k]["deps"] if not cover >> d & 1])
+        for d in pred[k]:
+            cover |= 1 << d
+        anc[k] = cover
+    succ = [[] for _ in range(n)]
+    for k in range(n):
+        for d in pred[k]:
+            succ[d].append(k)
+    cost = [x["c"] for x in nodes]; eng = [x["e"] for x in nodes]
+    full = [x["c"] + x["lat"] + HOP for x in nodes]
+
+    def run(order):
+        busy = {e: ([], [], []) for e in set(eng)}
+        st = [0.0] * n; fin = [0.0] * n; why = [-1] * n
+        for k in order:
+            t0 = 0.0; w = -1
+            for j in pred[k]:
+                if fin[j] > t0:
+                    t0 = fin[j]; w = j
+            d = cost[k]
+            if d > 0:
+                bs, be, bk = busy[eng[k]]
+                i = len(bs)
+                while i > 0 and be[i - 1] > t0:
+                    i -= 1
+                m = len(bs)
+                while i < m and t0 + d > bs[i] + 1e-9:
+                    if be[i] > t0:
+                        t0 = be[i]; w = -2 - bk[i]
+                    i += 1
+                bs.insert(i, t0); be.insert(i, t0 + d); bk.insert(i, k)
+            st[k] = t0; fin[k] = t0 + full[k]; why[k] = w
+        return st, fin, why
+
+    def legal(key):
+        key = list(key)
+        for k in range(n - 1, -1, -1):
+            for j in succ[k]:
+                if key[k] >= key[j]:
+                    key[k] = key[j] - 1e-6
+        return sorted(range(n), key=lambda z: key[z])
+    bl = [0.0] * n
+    for k in range(n - 1, -1, -1):
+        bl[k] = full[k] + max([bl[j] for j in succ[k]], default=0.0)
+    left = [len(p) for p in pred]; rt = [0.0] * n; free = {e: 0.0 for e in set(eng)}; st = [0.0] * n
+    ready = [k for k in range(n) if left[k] == 0]
+    while ready:
+        t0 = min(max(rt[k], free[eng[k]]) for k in ready)
+        k = max((z for z in ready if max(rt[z], free[eng[z]]) <= t0), key=lambda z: bl[z])
+        ready.remove(k)
+        st[k] = t0
+        if cost[k] > 0:
+            free[eng[k]] = t0 + cost[k]
+        for j in succ[k]:
+            rt[j] = max(rt[j], t0 + full[k]); left[j] -= 1
+            if left[j] == 0:
+                ready.append(j)
+    marks = [k for k in range(n) if nodes[k]["k"] == "a"]
+    score = lambda f: max(f) + 0.02 * sum(f[k] for k in marks) + 1e-4 * sum(f)
+    st, fin, why = run(legal(st))
+    cur = best = (score(fin), st, fin, why)
+    seed = [SEED]
+
+    def rnd():
+        seed[0] = (seed[0] * 1103515245 + 12345) % 2147483648
+        return seed[0] / 2147483648.0
+    for it in range(ROUNDS):
+        _, st, fin, why = cur
+        k = max(range(n), key=lambda z: fin[z])
+        arcs = []
+        while why[k] != -1:
+            if why[k] <= -2:
+                arcs.append((-2 - why[k], k)); k = -2 - why[k]
+            else:
+                k = why[k]
+        if not arcs:
+            break
+        key = list(st)
+        for _ in range(1 + int(rnd() * 2)):
+            u, v = arcs[int(rnd() * len(arcs))]
+            if rnd() < 0.5:
+                key[v] = key[u] - 1e-3 - rnd() * rnd() * 2.0
+            else:
+                key[u] = key[v] + 1e-3 + rnd() * rnd() * 2.0
+                stack = [u]
+                while stack:
+                    z = stack.pop()
+                    for j in succ[z]:
+                        if key[j] <= key[z]:
+                            key[j] = key[z] + 1e-6; stack.append(j)
+        s2, f2, w2 = run(legal(key))
+        sc = score(f2)
+        if sc < cur[0] + TEMP * (1.0 - it / ROUNDS) * rnd():
+            cur = (sc, s2, f2, w2)
+            if sc < best[0]:
+                best = cur
+    return legal(best[1]), best[1], max(best[2])
+
+
+ORDER = []
+
+
+def rank_program(g, core, T, topo):
+    if T.rank_of(core) is None:
+        return
+    nodes, nloc = build(g, core, T, topo)
+    if not ORDER:
+        ORDER.append(schedule(nodes)[0])
+    order = ORDER[0]
+    q = {"v": g.vector, "s": g.scalar, "t": g.tensor, "g": g, "y": g.sync}
+    count = {"v": 0, "s": 0, "t": 0, "g": 0}
+    clock = {e: {} for e in q}
+    done = {}
+    last = {}
+    for k in order:
+        x = nodes[k]
+        if x["k"] == "a":
+            done[k] = (x["sem"], x["cnt"], {})
+            last[x["sem"]] = x["cnt"]
+            continue
+        e = x["e"]; ck = clock[e]
+        need = [done[d] for d in x["deps"] if done[d] is not None]
+        need.sort(key=lambda z: -z[1])
+        for (sem, cnt, c2) in need:
+            if ck.get(sem, 0) < cnt and not any(z[2].get(sem, 0) >= cnt for z in need):
+                q[e].wait_ge(T.sem[sem], cnt)
+            ck[sem] = max(ck.get(sem, 0), cnt)
+            for s2, v2 in c2.items():
+                if ck.get(s2, 0) < v2:
+                    ck[s2] = v2
+        r = x["f"]()
+        if x["k"] == "c":
+            count[e] += 1
+            r.then_inc(T.sem["e" + e], 1)
+            done[k] = ("e" + e, count[e], dict(ck))
+            last["e" + e] = count[e]
+        elif x["k"] == "d":
+            done[k] = (x["sem"], x["cnt"], dict(ck))
+            last[x["sem"]] = x["cnt"]
+        else:
+            done[k] = None
+    last["loc"] = nloc
+    for sem, cnt in last.items():
+        g.wait_ge(T.sem[sem], cnt)

@@ -3,7 +3,8 @@ from concourse.mybir import AluOpType, ActivationFunctionType
 
 NS, L, NV, ST, DR = 3072, 192, 208, 5, 3
 O, ZC = 16, 224
-IDR, TZ, HB, TW = 400, 784, 992, 1184
+MU, SW, CP, HL, TW = 192, 208, 400, 608, 816
+KC, SH = 608, 416
 NO = 255 * 128
 F32, F16, BF, I32, U16 = "float32", "float16", "bfloat16", "int32", "uint16"
 
@@ -16,35 +17,40 @@ def _sb(names, cols, dtype):
 
 
 _sb("nbs", NS, I32); _sb("qw", NS + 16, BF); _sb("xq dd", 3344, BF); _sb("d0", 3344, F16)
-_sb("s0i", L, I32); _sb("usi coi", 960, I32); _sb("s0h", L, F16); _sb("ush coh", 960, F16)
-_sb("w0s lv", L, F32); _sb("lor hir", 8, F32); _sb("lh0 lh1", 16, F32)
+_sb("s0i", L, I32); _sb("usi coi", 960, I32); _sb("s0h dm", L, F16); _sb("ush coh", 960, F16)
+_sb("lor hir", 8, F32); _sb("lh0 lh1", 16, F32)
 _sb("ub", 16 + ST * NV, BF); _sb("nco", 960, BF)
 _sb("offq", NV, U16); _sb("nk16 h16 yy nkn", NV, F16); _sb("eqs", 5 * NV, F16); _sb("ge", NV, BF)
-_sb("wv0 wv1 wv2 wv3 wv4 wv5 w2 hw hf nkm", 240, F32); _sb("w1", 224, F32)
+_sb("wv0 wv1 wv2 wv3 wv4 wv5 w1 hw hf nkm", 240, F32)
 _sb("snd", 160, F32); _sb("cnt dif", 32, BF)
-_sb("nt", NV, F32); _sb("ti", NV, I32); _sb("mm", 608, F16); _sb("sg", 384, BF)
-_sb("fl", 32, F16); _sb("rr ga gb qa qb", 32, F32); _sb("so go soff aoff", 16, U16); _sb("srcw0 srcw1", 16, U16)
-_sb("tb", TW, BF); _sb("idv onesb", L, BF); _sb("srcb", 240, BF)
-_sb("nka eqa", 80, F16); _sb("asc", 16, F32); _sb("sm", 32, F32); _sb("junk", 192, F32)
+_sb("nt", NV, F32); _sb("ti", NV, I32); _sb("mm", 640, F16); _sb("mu", L, F32)
+_sb("fl kc", 48, F16); _sb("rr d0c", 48, F32); _sb("lst", 48, U16); _sb("soff aoff srcw0 srcw1", 32, U16)
+_sb("tb", TW, F32); _sb("srcb ssc", 224, BF); _sb("fh rc big", NV, F16); _sb("sur", 16, U16)
+_sb("nka eqa", 80, F16); _sb("asc", 16, F32); _sb("sm", 32, F32); _sb("junk", NV, F32)
 _sb("wo ho", NV, F32)
-_sb("jq", 256, F32); _sb("dq onef bt bf lf uf t1 t2 t3 t4 ba", 128, F32); _sb("pi", 8, I32); _sb("g8i", 144, I32); _sb("w8i", 144, I32)
-_sb("col", 32, F32); _sb("dg", 16, F32); _sb("da", 128, F32); _sb("jd db dc ds ssc", 240, BF); _sb("wsc", NV, F32); _sb("addc", 8, F32); _sb("jm cw idw", 16, F32); _sb("d0c", 32, F32)
-_sb("b16 i16 i4k trih uph trio upo r0 r1 r2 r3 r4 g8", 128, F16); _sb("f16 w8", 144, F16); _sb("fb", 144, BF)
-_sb("i2b bid ih iq i125", 128, BF); _sb("rw", 256, BF)
+_sb("jq", 256, F32); _sb("dq jb bf lf uf t1 t2 ba da", 128, F32); _sb("pi", 8, I32); _sb("g8i w8i", 144, I32)
+_sb("col", 32, F32); _sb("dg jm idw", 16, F32); _sb("jd db dc ds", 240, BF); _sb("wsc", NV, F32); _sb("addc", 8, F32)
+_sb("b16 i16 i2h i4k tri upp r0 r1 r2 r3 r4 g8 one", 128, F16); _sb("f16 w8", 144, F16); _sb("fb", 144, BF)
+_sb("i2b bid", 128, BF); _sb("rw", 256, BF)
 for _i in range(8):
     SCRATCH["p%d" % _i] = ("psum", [128, 512], F32)
 
 SEMAPHORES = (["ev", "es", "et", "eg", "loc"] + ["aw%d" % i for i in range(5)] + ["af%d" % i for i in range(4)]
               + ["dm%d" % i for i in range(12)])
 
-CH0 = [(0, 64), (64, 128), (128, 192)]
-CH1 = [(0, 64), (64, 128), (128, 208)]
-GA0 = [("v", 0, 32), ("s", 32, 64), ("s", 64, 128), ("s", 128, 192)]
-GA1 = [("v", 0, 32), ("s", 32, 64), ("s", 64, 128), ("s", 128, 192), ("v", 192, 208)]
-GA4 = [("v", 0, 64), ("s", 64, 128), ("s", 128, 192), ("v", 192, 208)]
-CY, PC, HOP = 0.00104, 0.0006, 0.10
-LINK = 2.5
-ROUNDS, TEMP, SEED = 20000, 0.2, 1
+GA = [("v", 0, 32), ("s", 32, 64), ("v", 64, 80), ("s", 80, 144), ("s", 144, 192), ("v", 192, 208)]
+PRE = [(0, 64), (64, 144), (144, 208)]
+POST = [(0, 64), (64, 144), (144, 208)]
+NK16 = [(0, 128), (128, 208)]
+OFFQ = [("v", 0, 192)]
+ENG = {"tb": "s", "h16": "s", "ha": "v", "nkn": "sss", "nka": "v", "fa": "v", "d0": "vvvv", "soff": "sss",
+       "aoff": "v", "offa": "v", "nk16": "s", "lst": "v", "srcw": "v"}
+COST = {"cy": 0.00095, "pc": 0.00055, "ga": 1.56, "sc": 3.8, "hop": 0.10, "link": 2.0, "dif": 4.0, "nb": 6.5, "q": 9.0}
+ROUNDS, TEMP, SEED, TURN, MARK = 35000, 0.4, 1, 0.3, 0.02
+
+
+def price(x, m):
+    return x["fx"] + m["cy"] * (x["cy"] + m["ga"] * x["ga"] + m["sc"] * x["sc"]) + m["pc"] * x["pe"]
 
 
 def build(g, core, T, topo):
@@ -64,7 +70,7 @@ def build(g, core, T, topo):
     def ind(win, off):
         return {"ap": win["ap"].indirect(off["ap"]), "r": win["r"], "o": off["r"], "n": 16 * off["n"], "m": "sbuf", "d": win["d"], "ind": 1}
 
-    def node(eng, fn, outs, ins, cost, extra=(), lat=0.0, kind="c", sem=None, cnt=0):
+    def node(eng, fn, outs, ins, cost, extra=(), lat=None, kind="c", sem=None, cnt=0):
         k = len(nodes)
         deps = set(extra)
         wr = []; rd = []
@@ -82,23 +88,36 @@ def build(g, core, T, topo):
                 if w and not ps:
                     acc[nm] = [z for z in acc[nm] if not (lo <= z[2] and z[3] <= hi)]
                 acc[nm].append((k, eng, lo, hi, w))
-        nodes.append({"e": eng, "f": fn, "deps": sorted(deps), "c": cost, "lat": lat, "k": kind, "sem": sem, "cnt": cnt, "nm": (wr[:1], rd[:2])})
+        x = {"fx": 0.0, "cy": 0, "ga": 0, "sc": 0, "pe": 0}
+        x.update(cost)
+        x.update({"e": eng, "f": fn, "deps": sorted(deps), "after": [], "lat": lat, "k": kind, "sem": sem, "cnt": cnt, "nm": (wr[:1], rd[:2])})
+        x["t"] = step[0]
+        nodes.append(x)
         return k
+
+    step = [None]
+
+    tail = {}
+
+    def chain(key, k):
+        if key in tail:
+            nodes[k]["after"].append(tail[key])
+        tail[key] = k
 
     def P(x):
         return x["ap"] if isinstance(x, dict) else x
 
-    def vc(out, ins, two=False):
+    def vc(out, ins, two=False, fx=0.05, fast=True):
         xs = [out] + [x for x in ins if isinstance(x, dict) and x["n"] > 1]
         n = max(x["n"] for x in xs)
         if out["ind"]:
-            return 0.05 + n * 3.8 * CY
+            return {"fx": fx, "sc": n}
         if any(x["ind"] for x in xs):
-            return 0.05 + n * 1.56 * CY
-        c = 0.5 if all(x["d"] in (F16, BF, U16) for x in xs) else 1.0
+            return {"fx": fx, "ga": n}
+        c = 0.5 if fast and all(x["d"] in (F16, BF, U16) for x in xs) else 1.0
         if two:
             c = 2.0 if all(x["m"] == "sbuf" for x in ins) else 1.0
-        return 0.05 + max(64, n * c) * CY
+        return {"fx": fx, "cy": max(64, n * c)}
 
     def ts(out, i0, s1, s2, op0, op1=None, extra=()):
         if op1 is None:
@@ -117,17 +136,30 @@ def build(g, core, T, topo):
         return node("v", lambda: g.vector.memset(P(out), c), [out], [], vc(out, []))
 
     def scan(out, d0, d1, init, op0, op1):
-        return node("v", lambda: g.vector.tensor_tensor_scan(P(out), P(d0), P(d1), init, op0, op1), [out], [d0, d1], vc(out, [d0, d1]))
+        return node("v", lambda: g.vector.tensor_tensor_scan(P(out), P(d0), P(d1), P(init), op0, op1), [out], [d0, d1, init], vc(out, [d0, d1]))
 
     def act(out, i0, func=None, bias=0.0, scale=1.0, accum=None, extra=()):
         func = AF.Identity if func is None else func
-        n = max(out["n"], i0["n"])
-        cost = 0.07 + (n * 1.56 if i0["ind"] else max(64, n)) * CY
+        cost = vc(out, [i0], fx=0.065 if accum is None else 0.085, fast=False)
+        if out["ind"]:
+            return node("s", lambda: g.scalar.activation(P(out), P(i0), func), [out], [i0], cost, extra)
         if accum is None:
             f = lambda: g.scalar.activation(P(out), P(i0), func, bias=P(bias), scale=P(scale))
             return node("s", f, [out], [i0, bias, scale], cost, extra)
         f = lambda: g.scalar.activation(P(out), P(i0), func, bias=P(bias), scale=P(scale), accum_out=P(accum))
-        return node("s", f, [out, accum], [i0, bias, scale], cost + 0.02, extra)
+        return node("s", f, [out, accum], [i0, bias, scale], cost, extra)
+
+    def lin(e, out, i0, scale=1.0, bias=0.0, extra=()):
+        if e == "s":
+            return act(out, i0, bias=bias, scale=scale, extra=extra)
+        if scale == 1.0 and bias == 0.0:
+            return cp(out, i0, extra)
+        return ts(out, i0, scale, bias, A.mult, A.add, extra)
+
+    def off(e, out, i0, bias):
+        if e == "s":
+            return act(out, i0, AF.Relu, bias=bias)
+        return ts(out, i0, bias, None, A.add)
 
     def mm(out, pairs, extra=()):
         def f():
@@ -136,28 +168,28 @@ def build(g, core, T, topo):
                 r = g.tensor.matmul(P(out), P(l), P(x), i == 0, i == len(pairs) - 1)
             return r
         ins = [z for pr in pairs for z in pr]
-        return node("t", f, [out], ins, 0.05 + len(pairs) * (max(64, out["n"]) * PC + 0.005), extra)
+        return node("t", f, [out], ins, {"fx": 0.05 + 0.005 * len(pairs), "pe": len(pairs) * max(64, out["n"])}, extra)
 
     def iota(out, pat, base, cm):
         if out["d"] == I32:
             f = lambda: g.iota(P(out), pat, base, cm)
         else:
             f = lambda: g.iota(P(out), pat, base, cm, allow_small_or_imprecise_dtypes=True)
-        return node("g", f, [out], [], 0.13 + 2 * out["n"] * CY)
+        return node("g", f, [out], [], {"fx": 0.13, "cy": 2 * out["n"]})
 
     def asel(out, i0, pat, op, fill, base, cm):
-        return node("g", lambda: g.affine_select(P(out), P(i0), pat, op, fill, base, cm), [out], [i0], 0.17 + 2 * out["n"] * CY)
+        return node("g", lambda: g.affine_select(P(out), P(i0), pat, op, fill, base, cm), [out], [i0], {"fx": 0.17, "cy": 2 * out["n"]})
 
     ndma = [0]
 
-    def dma(q, pairs, outs, ins, lat):
+    def dma(q, pairs, outs, ins, lat, extra=()):
         sem = "dm%d" % ndma[0]; ndma[0] += 1
         eng = g.sync if q == "y" else g.scalar
 
         def f():
             for o_, i_ in pairs:
                 eng.dma_start(o_, i_).then_inc(T.sem[sem], 16)
-        return node(q, f, outs, ins, 0.06 * len(pairs), lat=lat, kind="d", sem=sem, cnt=16 * len(pairs))
+        return node(q, f, outs, ins, {"fx": 0.06 * len(pairs)}, extra, lat=lat, kind="d", sem=sem, cnt=16 * len(pairs))
 
     sh = 16 * rank
 
@@ -172,20 +204,26 @@ def build(g, core, T, topo):
         return [(dst[sh:128, :], T[name][0:128 - sh, lo:hi]), (dst[0:sh, :], T[name][128 - sh:128, lo:hi])]
 
     dma("s", [(T.s0i[0:8, :], T.s0[:, :])], [a("s0i")], [], 2.0)
-    dma("y", rot_in("nbs", T.nb, 0, NS), [a("nbs")], [], 6.5)
-    dma("y", rot_in("qw", T.qs, 0, NS), [a("qw", 0, NS)], [], 9.0)
-    dma("s", rot_in("w0s", T.w0, 0, L), [a("w0s")], [], 3.0)
-    dma("s", [(T.usi[0:8, :], T.us[:, :]), (T.coi[0:8, :], T.coin[:, :])], [a("usi"), a("coi")], [], 3.0)
-    dma("s", rot_in("lor", T.lo, 0, ST) + rot_in("hir", T.hi, 0, ST), [a("lor"), a("hir")], [], 4.0)
+    dma("s", [(T.usi[0:8, :], T.us[:, :]), (T.coi[0:8, :], T.coin[:, :])], [a("usi"), a("coi")], [], 2.5)
+    dma("y", rot_in("nbs", T.nb, 0, NS), [a("nbs")], [], "nb")
+    dma("y", rot_in("qw", T.qs, 16, 16 + NS), [a("qw", 16, 16 + NS)], [], "q")
+    dma("y", rot_in("wv0", T.w0, 0, L), [a("wv0", 0, L)], [], "q")
+    dma("y", rot_in("lor", T.lo, 0, ST) + rot_in("hir", T.hi, 0, ST), [a("lor"), a("hir")], [], "q")
 
     c = lambda j: a("col", j, j + 1)
-    PM, P16, E15, TC, SC, THR, RM, RB, NTZ, AD, AD2, PM1, C200 = range(13)
-    iota(a("g8i", 0, 128, p=8), [[1, 8], [0, 16]], rank + 8, -1)
-    iota(a("w8i", p=8), [[1, 144]], 16 * rank + 240, -16)
+    PM, P16, E15, TC, SC, THR, RM, RB, AD, AD2, PM1, ID, R0 = range(13)
+
+    def fill(name, lo, hi, v):
+        for x in range(lo, hi, 256):
+            act(a(name, x, min(hi, x + 256)), a("jq", 0, min(hi, x + 256) - x), bias=v, scale=0.0)
     iota(a("pi", 0, 1), [[0, 1]], 0, 1)
+    iota(a("w8i", p=8), [[1, 144]], 16 * rank + 240, -16)
+    iota(a("g8i", 0, 128, p=8), [[1, 8], [0, 16]], rank + 8, -1)
     iota(a("jq"), [[1, 256]], 0, 0)
     iota(a("dq"), [[1, 128]], 0, -1)
+    iota(a("jb"), [[16, 8], [0, 16]], 0, 0)
     iota(a("jm"), [[16, 16]], 0, 0)
+    iota(a("jd"), [[0, 15], [1, 16]], 0, 0)
     ts(a("g8i", 0, 128, p=8), a("g8i", 0, 128, p=8), 7, None, A.bitwise_and)
     ts(a("g8", p=8), a("g8i", 0, 128, p=8), 0.0, None, A.is_equal)
     ts(a("w8i", p=8), a("w8i", p=8), 127, None, A.bitwise_and)
@@ -199,58 +237,51 @@ def build(g, core, T, topo):
     act(c(THR), c(E15), scale=16.0 * NO + 1280.0, bias=-16.0 * NO - 1216.0)
     ts(c(RM), c(PM), 5.5, None, A.is_lt)
     act(c(RB), c(RM), scale=1025.0, bias=-1.0)
-    act(c(NTZ), c(PM), scale=-1.0, bias=float(-TZ))
     act(c(AD), c(E15), scale=-8192.0, bias=9216.0)
     act(c(AD2), c(E15), scale=-256.0, bias=256.0)
     act(c(PM1), c(PM), bias=1.0)
-    act(c(C200), c(PM), bias=200.0)
-    ms(a("onef"), 1.0)
-    asel(a("bt"), a("onef"), [[16, 8], [0, 16]], A.is_ge, 0.0, 15, -1)
-    asel(a("bf"), a("bt"), [[-16, 8], [0, 16]], A.is_ge, 0.0, 0, 1)
+    act(c(ID), c(PM), bias=float(SH))
+    act(c(R0), c(PM), bias=-(L + 1) / 2.0, scale=-1.0)
+    fill("big", 0, NV, 1000.0); fill("fh", L, NV, 0.0)
+    ts(a("bf"), a("jb"), c(P16), None, A.is_equal)
+    act(a("b16"), a("bf"))
     asel(a("lf"), a("bf"), [[1, 128]], A.is_ge, 0.0, 0, -1)
     asel(a("uf"), a("bf"), [[-1, 128]], A.is_gt, 0.0, 0, 1)
-    for tmp, src, fill, dst in (("t1", "lf", TZ, "trih"), ("t2", "uf", 1 - TZ, "uph"), ("t3", "lf", HB, "trio"), ("t4", "uf", 1 - HB, "upo")):
-        asel(a(tmp), a(src), [[1, 128]], A.not_equal, float(fill), 0, -1)
-        cp(a(dst), a(tmp))
-    def fill(name, lo, hi, v):
-        for x in range(lo, hi, 256):
-            act(a(name, x, min(hi, x + 256)), a("jq", 0, min(hi, x + 256) - x), bias=v, scale=0.0)
-    cp(a("b16"), a("bf"))
-    ts(a("f16"), a("jq", 0, 144), c(P16), 16.0, A.subtract, A.is_equal)
+    for tmp, src, v, dst in (("t1", "lf", KC, "tri"), ("t2", "uf", 1 - KC, "upp")):
+        asel(a(tmp), a(src), [[1, 128]], A.not_equal, float(v), 0, -1)
+        act(a(dst), a(tmp))
     ts(a("fb"), a("jq", 0, 144), c(P16), 16.0, A.subtract, A.is_equal)
-    for nm, v in (("i16", 1.0), ("i4k", 4096.0)):
-        ts(a(nm), a("dq"), 0.0, v, A.is_equal, A.mult)
+    act(a("f16"), a("fb"))
     ts(a("rw", 0, 128), a("dq"), 0.0, None, A.is_equal)
     act(a("rw", 128, 256), a("rw", 0, 128))
-    for nm, v in (("i2b", 2.0 ** -6), ("ih", 0.5), ("iq", -0.25), ("i125", 1.25)):
+    for nm, v in (("i16", 1.0), ("i2h", 2.0), ("i4k", -4096.0), ("i2b", 2.0 ** -6)):
         act(a(nm), a("rw", 0, 128), scale=v)
     ts(a("ba"), a("dq"), c(TC), c(SC), A.is_equal, A.mult)
-    tt(a("bid"), a("ba"), a("ih"), A.add)
+    asel(a("bid"), a("ba"), [[1, 128]], A.not_equal, 0.5, 0, -1)
     ts(a("dg"), a("jq", 0, 16), c(PM), None, A.is_equal)
     for p in range(5):
-        ts(a("r%d" % p), a("b16"), a("dg", p, p + 1), None, A.mult)
-    iota(a("jd"), [[0, 15], [1, 16]], 0, 0)
+        act(a("r%d" % p), a("bf"), scale=a("dg", p, p + 1))
     ts(a("db"), a("jd"), c(PM1), -256.0, A.is_equal, A.mult)
     ts(a("dc"), a("jd"), c(PM), 2048.0, A.is_equal, A.mult)
     tt(a("ds"), a("dc"), a("db"), A.add)
     act(a("da"), a("ds", 0, 128), scale=32.0)
-    act(a("addc"), a("onef", 0, 8), scale=c(AD))
-    act(a("cw"), a("jm"), bias=c(C200))
-    act(a("idw"), a("cw"), bias=float(IDR - 200))
-    ts(a("go", 13, 15), a("onef", 0, 2), c(PM), float(HB - 1), A.add, A.add)
-    fill("tb", 0, IDR, 0.0); fill("tb", IDR + L, TW, float(ZC))
-    act(a("tb", IDR, IDR + L), a("jq", 0, L), bias=float(O))
-    act(a("idv"), a("jq", 0, L), bias=float(O))
-    fill("onesb", 0, L, 1.0)
-    fill("d0c", 0, 13, 1.0); fill("d0c", 13, 14, 0.0); fill("d0c", 14, 26, 1.0)
+    act(a("addc"), a("jq", 0, 8), scale=0.0, bias=c(AD))
+    act(a("idw"), a("jm"), bias=c(ID))
+    act(a("tb", 0, L), a("jq", O, O + L), AF.Silu if ENG["tb"] == "s" else AF.Identity)
+    ms(a("tb", MU, SW), 1.0); ms(a("tb", MU + 1, MU + 2), 2.0); ms(a("tb", MU + 2, MU + 3), 0.5)
+    fill("tb", SW, CP, 0.0)
+    fill("one", 0, 128, 1.0)
+    ms(a("kc"), 0.0); ms(a("kc", 12, 13), float(SH)); ms(a("kc", 14, 28, 13), float(SW)); ms(a("kc", 28, 40), float(SH + MU))
+    ms(a("d0c"), 1.0); ms(a("d0c", 14, 15), 0.0); ms(a("d0c", 28, 40), 0.0)
     ms(a("fl", 0, 1), 0.0)
-    ms(a("mm", 192, 208), 0.0); ms(a("mm", 400, 416), 1.0)
+    for x in (L, NV + 16 + L):
+        fill("mm", x, x + 16, 1.0); fill("mm", x + 16, x + 32, 0.0)
     for x in range(0, 3344, 836):
         ms(a("d0", x, x + 836), 60000.0)
     fill("xq", 0, 16, float(NO))
-    fill("qw", NS, NS + 16, 0.0)
+    fill("qw", 0, 16, 0.0)
     fill("ub", 0, O, 0.0); fill("ub", NV, NV + O, 0.0)
-    fill("w1", 0, O, 0.0); fill("w2", 0, 240, 0.0); fill("hw", 0, 240, 0.0); fill("hf", 0, 240, -1.0); fill("nkm", 0, 240, 2048.0)
+    fill("w1", 0, 240, 0.0); fill("hw", 0, 240, 0.0); fill("hf", 0, 240, -1.0); fill("nkm", 0, 240, -4096.0)
     fill("wo", 0, O, 0.0); fill("ho", 0, O, 0.0)
     E = lambda k: a("f16", 16 - k, 144 - k)
     EB = lambda k: a("fb", 16 - k, 144 - k)
@@ -263,25 +294,24 @@ def build(g, core, T, topo):
         mm(a(pb, L, 2 * L), [(a("g8", p=8), a("coh", t * L, t * L + L, p=8))])
         act(a("ub", O + t * NV, O + t * NV + L), a(pb, 0, L))
         act(a("nco", t * L, t * L + L), a(pb, L, 2 * L))
+    fill("lh0", 0, 16, 0.0)
     act(a("lh0", 0, ST), a("lor", 0, ST)); act(a("lh0", 8, 8 + ST), a("hir", 0, ST))
-    fill("lh0", 5, 8, 0.0); fill("lh0", 13, 16, 0.0)
 
     ts(a("s0h", p=8), a("s0i", p=8), -1024.0, None, A.add)
     mm(a("p6", 0, 12), [(a("w8", 16 - r, 144 - r, p=8), a("s0h", r, L, 16, p=8)) for r in range(16)])
     ts(a("soff", 0, 12), a("p6", 0, 12), 1024.0, None, A.add)
     mm(a("p3", 0, L), [(a("g8", p=8), a("s0h", p=8))])
     mm(a("p4", 0, L), [(a("w8", 16, 144, p=8), a("s0h", p=8))])
+    ts(a("dm"), a("p3", 0, L), -1024.5, None, A.is_lt)
     ts(a("nkn", 0, L), ind(a("nbs"), a("soff", 0, 12)), -1024.0, None, A.add)
     tt(a("eqs", 0, L), a("nkn", 0, L), a("p3", 0, L), A.is_equal)
-    mm(a("p7", 0, L), [(a("i16"), a("nkn", 0, L)), (a("i4k"), a("eqs", 0, L))])
-    ts(a("offq", 0, L), a("p7", 0, L), 1024.0, 3072.0, A.add, A.min)
-    cp(a("h16", 0, L), a("p4", 0, L))
-    ts(a("lv"), a("p3", 0, L), -1024.5, None, A.is_gt)
-    tt(a("wv0", 0, L), a("w0s"), a("lv"), A.mult)
+    mm(a("p7", 0, L), [(a("i4k"), a("dm")), (a("i16"), a("nkn", 0, L)), (a("i4k"), a("eqs", 0, L))])
+    off("v", a("offq", 0, L), a("p7", 0, L), 1040.0)
+    act(a("h16", 0, L), a("p4", 0, L))
     s = lambda j: a("sm", j, j + 1)
-    PD, YY, NVA, SG, FA = range(5)
-    act(a("junk"), a("lv"), accum=s(NVA))
-    act(s(PD), s(NVA), bias=float(L), scale=-1.0)
+    PD, YY, NVA, SG, FA, NH, NC = range(7)
+    act(a("junk", 0, L), a("p3", 0, L), AF.Sign, bias=1024.5, accum=s(NVA))
+    act(s(PD), s(NVA), bias=L / 2.0, scale=-0.5)
 
     peers = [T.cores[(rank + d) % n_r] for d in range(1, n_r)]
     nxt = T.cores[(rank + DR) % n_r]
@@ -289,22 +319,24 @@ def build(g, core, T, topo):
     arr_w = None; arr_f = None
     lh = "lh0"
     for t in range(ST):
+        step[0] = t
         nv = L if t == 0 else NV
         last = t == ST - 1
         wv = "wv%d" % t
         uo = O + t * NV
         hw = "hf" if last else "hw"
+        cut = lambda ch: [z[:-1] + (min(z[-1], nv),) for z in ch if z[-2] < nv]
         if t > 0:
             k = t + 1
-            cp(a("h16", L, NV), a(wv, NV, 224), extra=[arr_w])
-            for p in range(k):
+            lin(ENG["ha"], a("h16", L, NV), a(wv, NV, 224), extra=[arr_w])
+            for p in range(k - 1, -1, -1):
                 mm(a("p7", 256 + 16 * p, 272 + 16 * p), [(a("r%d" % p), a("h16", L, NV))])
             scan(a("asc"), a("da", 0, 16), a("p7", 256 + 16 * t, 272 + 16 * t), 0.0, A.add, A.min)
-            ts(a("aoff", 0, k), a("addc", 0, k), a("asc", 15, 16), 3071.0, A.add, A.min)
-            ts(a("nka", 0, 16 * k), ind(a("nbs"), a("aoff", 0, k)), -1024.0, None, A.add)
+            off(ENG["aoff"], a("aoff", 0, k), a("addc", 0, k), a("asc", 15, 16))
+            lin(ENG["nka"], a("nka", 0, 16 * k), ind(a("nbs"), a("aoff", 0, k)), bias=-1024.0)
             tt(a("eqa", 0, 16 * k), a("nka", 0, 16 * k), a("p7", 256, 256 + 16 * k), A.is_equal)
             mm(a("p7", 352, 368), [(a("i16"), a("nka", 0, 16))] + [(a("i4k"), a("eqa", 16 * p, 16 * p + 16)) for p in range(k)])
-            ts(a("offq", L, NV), a("p7", 352, 368), 1024.0, 3072.0, A.add, A.min)
+            off(ENG["offa"], a("offq", L, NV), a("p7", 352, 368), 1040.0)
             act(a("junk", 0, 16), a(wv, L, NV), AF.Sign, accum=s(NVA), extra=[arr_w])
             act(s(PD), s(NVA), AF.Relu, bias=s(YY), scale=-1.0)
             prs = [(a("rw", 0, 128), a("dif", 8 * t - 8, 8 * t - 7))]
@@ -312,54 +344,61 @@ def build(g, core, T, topo):
                 r2 = 8 * t - 8 + (rank + d) % n_r
                 prs.append((a("rw", 128 - 16 * d, 256 - 16 * d), a("cnt", r2, r2 + 1)))
             mm(a("p5", 300, 301), prs, extra=[arr_f])
-            act(s(SG), a("p5", 300, 301), AF.Sign, bias=-0.5)
-            act(s(FA), s(SG), bias=1.5, scale=0.5)
+            if ENG["fa"] == "s":
+                act(s(SG), a("p5", 300, 301), AF.Sign, bias=-0.5)
+                act(s(FA), s(SG), bias=1.5, scale=0.5)
+            else:
+                ts(s(FA), a("p5", 300, 301), 0.5, 1.0, A.is_gt, A.add)
             lh2 = "lh%d" % (t % 2)
             act(a(lh2), a(lh), scale=s(FA))
             lh = lh2
-        ts(a("nk16", 0, 128), a("offq", 0, 128), -1024.0, None, A.add)
-        ts(a("nk16", 128, nv), a("offq", 128, nv), -1024.0, None, A.add)
+        for (lo, hi) in cut(NK16):
+            lin(ENG["nk16"], a("nk16", lo, hi), a("offq", lo, hi), bias=-1040.0)
         act(a("p5", 0, L), a("nco", t * L, t * L + L), bias=2.0 ** -120, scale=a(lh, t, t + 1))
-        iota(a("tb", HB, HB + 16), [[1, 16]], 0, 0)
+        iota(a("tb", CP, TW), [[-ZC, 2], [0, 13], [1, 16]], ZC, 0)
         if not last:
             for p in range(t + 1):
                 mm(a("p%d" % (3 + p // 2), NV * (p % 2), NV * (p % 2) + nv), [(a("r%d" % p), a("h16", 0, nv))])
-        prev = []
-        for (e, lo, hi) in (GA0 if t == 0 else GA4 if last else GA1):
-            src = ind(a("qw"), a("offq", lo, hi))
-            if e == "v":
-                ts(a("xq", 16 * lo + 16, 16 * hi + 16), src, 2.0 ** -5, None, A.mult)
-            else:
-                prev = [act(a("xq", 16 * lo + 16, 16 * hi + 16), src, scale=2.0 ** -5, extra=prev)]
-        prev = []
-        for ci, (lo, hi) in enumerate(CH0 if t == 0 else CH1):
-            n = hi - lo
+        for (e, lo, hi) in cut(GA):
+            chain("g" + e, lin(e, a("xq", 16 * lo + 16, 16 * hi + 16), ind(a("qw"), a("offq", lo, hi)), scale=2.0 ** -5))
+        for ci, (b0, b1) in enumerate(cut(POST)):
             bank = "p%d" % ci
+            for pi_, (lo, hi) in enumerate(cut(PRE)):
+                if not b0 <= lo < b1:
+                    continue
+                pb = a(bank, lo - b0, hi - b0)
+                x0, x1 = 16 * lo + 16, 16 * hi + 16
+                chain("sum", mm(pb, [(a("i2b"), a("xq", x0 + k, x1, 16)) for k in range(16)]))
+                iota(a("xq", x0 + 15, x1, 16), [[0, hi - lo]], NO, 0)
+                tt(a("nt", lo, hi), pb, a("ub", uo + lo, uo + hi), A.mult)
+                tt(a("w1", O + lo, O + hi), pb, a(wv, lo, hi), A.mult, extra=[arr_w] if hi > L else [])
+                if ENG["d0"][pi_] == "v":
+                    ts(a("ti", lo, hi), a("nt", lo, hi), 2047.0 + 255.0 / 512.0, None, A.add)
+                    ts(a("d0", x0 - 1, x1 - 1, 16), a("ti", lo, hi), 2.0 ** -5, None, A.mult)
+                else:
+                    ts(a("nt", lo, hi), a("nt", lo, hi), 2047.0 + 255.0 / 512.0, 1.5 * 2 ** 23, A.add, A.add)
+                    act(a("d0", x0 - 1, x1 - 1, 16), a("nt", lo, hi), scale=2.0 ** -5, bias=-1.5 * 2 ** 18)
+                chain("scan", scan(a("dd", x0 - 1, x1 - 1), a("d0", x0 - 1, x1 - 1), a("xq", x0 - 1, x1 - 1), 60000.0, A.min, A.add))
+                mm(a(bank, 128 + lo - b0, 128 + hi - b0), [(EB(k), a("dd", x0 + k, x1 - 1, 16)) for k in range(15)])
+            lo, hi = b0, b1
+            n = hi - lo
             pb = a(bank, 0, n)
-            x0, x1 = 16 * lo + 16, 16 * hi + 16
-            mm(pb, [(a("i2b"), a("xq", x0 + k, x1, 16)) for k in range(16)])
-            iota(a("xq", x0 + 15, x1, 16), [[0, hi - lo]], NO, 0)
-            tt(a("nt", lo, hi), pb, a("ub", uo + lo, uo + hi), A.mult)
-            tt(a("w1", O + lo, O + hi), pb, a(wv, lo, hi), A.mult, extra=[arr_w] if hi > L else [])
-            ts(a("ti", lo, hi), a("nt", lo, hi), 2047.0 + 255.0 / 512.0, None, A.add)
-            ts(a("d0", x0 - 1, x1 - 1, 16), a("ti", lo, hi), 2.0 ** -5, None, A.mult)
-            scan(a("dd", x0 - 1, x1 - 1), a("d0", x0 - 1, x1 - 1), a("xq", x0 - 1, x1 - 1), 60000.0, A.min, A.add)
-            mm(a(bank, 128, 128 + n), [(EB(k), a("dd", x0 + k, x1 - 1, 16)) for k in range(15)])
             act(a("ge", lo, hi), a(bank, 128, 128 + n), AF.Sign, bias=c(THR))
             mm(pb, [(a("bid"), a("ge", lo, hi))])
             yy = a("yy", lo, hi)
             tt(yy, pb, a("nk16", lo, hi), A.mult)
             if not last:
                 mm(a(bank, 256, 256 + n), [(a("b16"), yy)])
-            hn = mm(a(bank, 384, 384 + n), [(a("i16"), a("h16", lo, hi)), (E(t + 1), yy)])
+            mm(a(bank, 384, 384 + n), [(a("i16"), a("h16", lo, hi)), (E(t + 1), yy)])
             if last:
                 act(a(hw, O + lo, O + hi), a(bank, 384, 384 + n), bias=c(RB), scale=c(RM))
                 continue
-            act(a(hw, O + lo, O + hi), a(bank, 384, 384 + n))
             scan(a("wsc", lo, hi), a("da", 0, n), a(bank, 256, 256 + n), 0.0, A.add, A.min)
-            ts(a("soff", lo // 16, hi // 16), a("wsc", lo + 15, hi, 16), c(AD), 3071.0, A.add, A.min)
+            act(a(hw, O + lo, O + hi), a(bank, 384, 384 + n))
+            so = a("soff", 8 * ci, 8 * ci + n // 16)
+            off(ENG["soff"][ci], so, a("wsc", lo + 15, hi, 16), c(AD))
             nk = a("nkn", lo, hi)
-            ts(nk, ind(a("nbs"), a("soff", lo // 16, hi // 16)), -1024.0, None, A.add)
+            lin(ENG["nkn"][ci], nk, ind(a("nbs"), so), bias=-1024.0)
             terms = [(a("i16"), nk)]
             for p in range(t + 2):
                 hb = a(bank, 256, 256 + n) if p == t + 1 else a("p%d" % (3 + p // 2), NV * (p % 2) + lo, NV * (p % 2) + hi)
@@ -367,71 +406,75 @@ def build(g, core, T, topo):
                 terms.append((a("i4k"), a("eqs", NV * p + lo, NV * p + hi)))
             mm(a(bank, 128, 128 + n), terms)
             act(a("nkm", O + lo, O + hi), a(bank, 128, 128 + n))
-        dst = a("srcw%d" % ((t + 1) % 2), 14, 15)
+        dst = a("srcw%d" % ((t + 1) % 2), 0, 1)
         if t > 0:
             cp(ind(a("w1", 0, NV), dst), a("w1", NV, NV + 16))
         w1 = a("w1", O, O + L)
         ts(a("mm", 0, L), w1, a(lh, 8 + t, 9 + t), None, A.is_gt)
-        tt(a("mm", NV, NV + L), w1, a("p5", 0, L), A.is_lt)
-        ts(a("mm", 416, 608), w1, a(lh, t, t + 1), None, A.is_lt)
-        mm(a("p5", 200, 226), [(E(r), a("mm", r, 416, 16)) for r in range(16)])
-        ts(a("fl", 1, 27), a("p5", 200, 226), 9.5, None, A.is_gt)
-        mm(a("p5", 230, 243), [(a("trih"), a("fl", 1, 14)), (a("uph"), a("fl", 0, 13))])
-        mm(a("p5", 243, 256), [(a("trio"), a("fl", 14, 27)), (a("upo"), a("fl", 13, 26))])
-        scan(a("rr", 0, 26), a("d0c", 0, 26), a("p5", 230, 256), 0.0, A.mult, A.add)
-        nc = a("rr", 12, 13)
-        tt(a("qa", 0, 12), a("rr", 13, 25), a("cw", 0, 12), A.max)
-        tt(a("qb", 0, 12), a("qa", 0, 12), a("rr", 0, 12), A.max)
-        ts(a("so", 0, 12), a("qb", 0, 12), nc, None, A.subtract)
-        ts(a("ga", 0, 13), a("rr", 13, 26), nc, float(TZ - HB), A.subtract, A.add)
-        tt(a("gb", 0, 13), a("ga", 0, 13), a("idw", 0, 13), A.max)
-        ts(a("go", 0, 13), a("gb", 0, 13), float(TZ), None, A.min)
-        cp(ind(a("tb"), a("so", 0, 12)), a("idv"))
-        act(a("srcb"), ind(a("tb"), a("go", 0, 15)))
-        mm(a("p6", 0, L), [(a("b16"), a("mm", 0, L))])
-        mm(a("p6", L, 2 * L), [(a("b16"), a("mm", 416, 608))])
-        act(a("sg"), a("p6", 0, 2 * L), AF.Sign, bias=-9.5)
-        mm(a("p7", 0, L), [(a("iq"), a("sg", 0, L)), (a("ih"), a("sg", L, 2 * L)), (a("i125"), a("onesb"))])
-        tt(a("w2", O, O + L), w1, a("p7", 0, L), A.mult)
+        tt(a("mm", 224, 224 + L), w1, a("p5", 0, L), A.is_lt)
+        ts(a("mm", 448, 640), w1, a(lh, t, t + 1), None, A.is_lt)
+        mm(a("p5", 304, 496), [(a("b16"), a("mm", 0, L))])
+        mm(a("p5", 0, L), [(a("b16"), a("mm", 224, 224 + L))])
+        ts(a("fh", 0, L), a("p5", 304, 496), 9.5, None, A.is_gt)
+        act(a("junk", 0, L), a("p5", 0, L), AF.Sign, bias=-9.5, accum=s(NH))
+        scan(a("rc"), a("fh"), a("big"), c(R0), A.add, A.min)
+        act(a("junk"), a("rc"), AF.Sign, bias=s(NH), scale=-2.0, accum=s(NC))
+        sur = a("sur", 2 * t, 2 * t + 1)
+        ts(sur, s(NC), 0.5, float(NV // 2 + O), A.mult, A.add)
+        mm(a("p6", 0, 40), [(E(r), a("mm", r, 640, 16)) for r in range(16)])
+        ts(a("fl", 1, 41), a("p6", 0, 40), 9.5, None, A.is_gt)
+        one = a("one", p=1)
+        mm(a("p6", 64, 92), [(one, a("kc", 0, 28, p=1)), (a("tri"), a("fl", 1, 29)), (a("upp"), a("fl", 0, 28))])
+        mm(a("p6", 92, 104), [(one, a("kc", 28, 40, p=1)), (a("i16"), a("fl", 29, 41)), (a("i16"), a("fl", 15, 27)), (a("i2h"), a("fl", 1, 13))])
+        scan(a("rr", 0, 40), a("d0c", 0, 40), a("p6", 64, 104), 0.0, A.mult, A.add)
+        tt(a("rr", 14, 26), a("rr", 14, 26), a("idw", 0, 12), A.max)
+        tt(a("rr", 0, 12), a("rr", 0, 12), a("rr", 14, 26), A.max)
+        off(ENG["lst"], a("lst", 0, 40), a("rr", 0, 40), float(-SH))
+        if ENG["tb"] == "s":
+            act(ind(a("tb", SW, TW), a("lst", 0, 12)), a("tb", 0, L), AF.Silu)
+        else:
+            cp(ind(a("tb", SW, TW), a("lst", 0, 12)), a("tb", 0, L))
+        act(a("srcb"), ind(a("tb"), a("lst", 12, 26)))
+        act(a("mu"), ind(a("tb", 0, SW), a("lst", 28, 40)))
         if t > 0:
             if not last:
                 cp(ind(a("nkm", 0, NV), dst), a("nkm", NV, NV + 16))
             cp(ind(a(hw, 0, NV), dst), a(hw, NV, NV + 16))
-        scan(a("ssc"), a("ds"), a("srcb"), 0.0, A.add, A.min)
+        scan(a("ssc"), a("ds", 0, 224), a("srcb"), 0.0, A.add, A.min)
         sw = "srcw%d" % (t % 2)
-        ts(a(sw, 0, 15), a("ssc", 15, 240, 16), c(AD2), None, A.add)
-        src = a(sw, 0, 12); sur = a(sw, 12, 13); dst = a(sw, 14, 15)
+        off(ENG["srcw"], a(sw, 0, 14), a("ssc", 15, 224, 16), c(AD2))
+        dst = a(sw, 0, 1); src = a(sw, 2, 14)
         so_ = 32 * t; wn = "wv%d" % (t + 1)
         if not last:
-            ts(a("offq", 0, L), ind(a("nkm"), src), 1024.0, 3072.0, A.add, A.min)
-        act(a("snd", so_, so_ + 16), ind(a("w2"), sur))
+            for (e, lo, hi) in OFFQ:
+                off(e, a("offq", lo, hi), ind(a("nkm"), a(sw, 2 + lo // 16, 2 + hi // 16)), 1040.0)
+        act(a("snd", so_, so_ + 16), ind(a("w1"), sur), scale=0.5)
         act(a("snd", so_ + 16, so_ + 32), ind(a(hw), sur))
         rid, pid, _ = topo.addr(nxt)
-        en = topo.engines(core, nxt)
-        ne = len(en) // 2
-        msk = sum(1 << x for x in en[:ne])
+        msk = topo.mask(core, nxt)
+        ne = len(topo.engines(core, nxt))
 
         def send(so_=so_, wn=wn, t=t, rid=rid, pid=pid, msk=msk):
             g.remote_dma(T[wn][:, L:224], T.snd[:, so_:so_ + 32], T.sem["aw%d" % t], T.sem.loc, pid, rid, msk)
-        sn = node("g", send, [], [a("snd", so_, so_ + 32)], 0.3, kind="r")
+        sn = node("g", send, [], [a("snd", so_, so_ + 32)], {"fx": 0.3}, kind="r")
         nloc[0] += ne
-        arr_w = node("x", None, [], [], 0.0, extra=[sn], lat=LINK, kind="a", sem="aw%d" % t, cnt=ne)
+        arr_w = node("x", None, [], [], {}, extra=[sn], lat="link", kind="a", sem="aw%d" % t, cnt=ne)
         if last:
-            cp(a("wo", O, NV), ind(a("w2"), src))
+            tt(a("wo", O, NV), ind(a("w1"), src), a("mu"), A.mult)
             act(a("ho", O, NV), ind(a(hw), src))
             cp(ind(a("wo"), dst), a(wn, L, NV), extra=[arr_w])
             cp(ind(a("ho"), dst), a(wn, NV, 224), extra=[arr_w])
             dma("y", rot_out(T.yw, "wo", O, NV), [], [a("wo")], 2.0)
             dma("s", rot_out(T.yh, "ho", O, NV), [], [a("ho")], 2.0)
         else:
-            act(a(wn, 0, L), ind(a("w2"), src))
-            cp(a("h16", 0, L), ind(a(hw), src))
+            tt(a(wn, 0, L), ind(a("w1"), src), a("mu"), A.mult)
+            lin(ENG["h16"], a("h16", 0, L), ind(a(hw), src))
             uo2 = uo + NV
             act(a("ub", uo2 + L, uo2 + NV), ind(a("ub", uo2 - O, uo2 + L), dst))
-            act(s(YY), a("ga", 12, 13), bias=c(NTZ))
+            act(s(YY), a("rr", 13, 14), bias=a("rr", 27, 28), scale=-1.0)
             dif = a("dif", 8 * t, 8 * t + 1)
             act(dif, s(YY), bias=s(PD), scale=-1.0)
-            m7 = sum(1 << x for x in en[ne:])
+            m7 = msk
             for q in peers:
                 m7 = m7 & topo.mask(core, q)
             n7 = bin(m7).count("1")
@@ -441,9 +484,10 @@ def build(g, core, T, topo):
                 tr = RemoteDMATransfer(dst_ids=ids, dma_engine_mask=m7, remote_sem=T.sem["af%d" % t], srcs=[dif["ap"]],
                                        dsts=[T.cnt[:, 8 * t + rank:8 * t + rank + 1] for q in peers])
                 g.remote_dma_fused([tr], local_sem=T.sem.loc)
-            sf = node("g", sendf, [], [dif], 0.5, kind="r")
+            sf = node("g", sendf, [], [dif], {"fx": 0.5}, kind="r")
+            nodes[sf]["after"].append(sn)
             nloc[0] += n7
-            arr_f = node("x", None, [], [], 0.0, extra=[sf], lat=LINK + 4.5, kind="a", sem="af%d" % t, cnt=n7 * (n_r - 1))
+            arr_f = node("x", None, [], [], {}, extra=[sf], lat="dif", kind="a", sem="af%d" % t, cnt=n7 * (n_r - 1))
     return nodes, nloc[0]
 
 
@@ -452,106 +496,108 @@ def schedule(nodes):
     anc = [0] * n
     pred = []
     for k in range(n):
+        deps = nodes[k]["deps"] + nodes[k]["after"]
         cover = 0
-        for d in nodes[k]["deps"]:
+        for d in deps:
             cover |= anc[d]
-        pred.append([d for d in nodes[k]["deps"] if not cover >> d & 1])
+        pred.append(sorted(set(d for d in deps if not cover >> d & 1)))
         for d in pred[k]:
             cover |= 1 << d
         anc[k] = cover
-    succ = [[] for _ in range(n)]
+    cost = [price(x, COST) for x in nodes]; eng = [x["e"] for x in nodes]
+    lag = [COST.get(x["lat"], x["lat"] or 0.0) + COST["hop"] for x in nodes]
+    arc = [[(d, lag[d] if d in nodes[k]["deps"] else 0.0) for d in pred[k]] for k in range(n)]
+    rev = [[] for _ in range(n)]
     for k in range(n):
-        for d in pred[k]:
-            succ[d].append(k)
-    cost = [x["c"] for x in nodes]; eng = [x["e"] for x in nodes]
-    full = [x["c"] + x["lat"] + HOP for x in nodes]
+        for d, w in arc[k]:
+            rev[d].append((k, w))
+    back = range(n - 1, -1, -1)
+    ends = [k for k in range(n) if not rev[k]]
+    marks = [k for k in range(n) if nodes[k]["k"] == "a"]
 
-    def run(order):
+    def run(order, arcs):
         busy = {e: ([], [], []) for e in set(eng)}
         st = [0.0] * n; fin = [0.0] * n; why = [-1] * n
         for k in order:
-            t0 = 0.0; w = -1
-            for j in pred[k]:
-                if fin[j] > t0:
-                    t0 = fin[j]; w = j
+            t0 = lag[k] if arcs is rev and not arcs[k] else 0.0
+            y = -1
+            for j, w in arcs[k]:
+                if fin[j] + w > t0:
+                    t0 = fin[j] + w; y = j
             d = cost[k]
             if d > 0:
                 bs, be, bk = busy[eng[k]]
-                i = len(bs)
+                i = m = len(bs)
                 while i > 0 and be[i - 1] > t0:
                     i -= 1
-                m = len(bs)
                 while i < m and t0 + d > bs[i] + 1e-9:
                     if be[i] > t0:
-                        t0 = be[i]; w = -2 - bk[i]
+                        t0 = be[i]; y = -2 - bk[i]
                     i += 1
                 bs.insert(i, t0); be.insert(i, t0 + d); bk.insert(i, k)
-            st[k] = t0; fin[k] = t0 + full[k]; why[k] = w
+            st[k] = t0; fin[k] = t0 + d; why[k] = y
         return st, fin, why
 
-    def legal(key):
+    def legal(key, turn=False):
         key = list(key)
-        for k in range(n - 1, -1, -1):
-            for j in succ[k]:
+        nxt = arc if turn else rev
+        for k in (range(n) if turn else back):
+            for j, _ in nxt[k]:
                 if key[k] >= key[j]:
                     key[k] = key[j] - 1e-6
         return sorted(range(n), key=lambda z: key[z])
-    bl = [0.0] * n
-    for k in range(n - 1, -1, -1):
-        bl[k] = full[k] + max([bl[j] for j in succ[k]], default=0.0)
-    left = [len(p) for p in pred]; rt = [0.0] * n; free = {e: 0.0 for e in set(eng)}; st = [0.0] * n
-    ready = [k for k in range(n) if left[k] == 0]
-    while ready:
-        t0 = min(max(rt[k], free[eng[k]]) for k in ready)
-        k = max((z for z in ready if max(rt[z], free[eng[z]]) <= t0), key=lambda z: bl[z])
-        ready.remove(k)
-        st[k] = t0
-        if cost[k] > 0:
-            free[eng[k]] = t0 + cost[k]
-        for j in succ[k]:
-            rt[j] = max(rt[j], t0 + full[k]); left[j] -= 1
-            if left[j] == 0:
-                ready.append(j)
-    marks = [k for k in range(n) if nodes[k]["k"] == "a"]
-    score = lambda f: max(f) + 0.02 * sum(f[k] for k in marks) + 1e-4 * sum(f)
-    st, fin, why = run(legal(st))
-    cur = best = (score(fin), st, fin, why)
+
+    def fore(key):
+        st, fin, why = run(legal(key), arc)
+        k = max(ends, key=lambda z: fin[z] + lag[z])
+        end = fin[k] + lag[k]
+        pairs = []
+        while why[k] != -1:
+            if why[k] <= -2:
+                pairs.append((-2 - why[k], k)); k = -2 - why[k]
+            else:
+                k = why[k]
+        return (end + MARK * sum(fin[z] for z in marks) + 1e-5 * sum(fin), st, end, pairs, fin)
+
+    def turn(c):
+        return fore([-z for z in run(legal([-z for z in c[4]], True), rev)[1]])
     seed = [SEED]
 
     def rnd():
         seed[0] = (seed[0] * 1103515245 + 12345) % 2147483648
         return seed[0] / 2147483648.0
+    bl = [0.0] * n
+    for k in back:
+        bl[k] = cost[k] + max([bl[j] + w for j, w in rev[k]], default=lag[k])
+    cur = best = turn(turn(fore([-x for x in bl])))
     for it in range(ROUNDS):
-        _, st, fin, why = cur
-        k = max(range(n), key=lambda z: fin[z])
-        arcs = []
-        while why[k] != -1:
-            if why[k] <= -2:
-                arcs.append((-2 - why[k], k)); k = -2 - why[k]
-            else:
-                k = why[k]
-        if not arcs:
-            break
-        key = list(st)
+        key = list(cur[1])
         for _ in range(1 + int(rnd() * 2)):
-            u, v = arcs[int(rnd() * len(arcs))]
-            if rnd() < 0.5:
-                key[v] = key[u] - 1e-3 - rnd() * rnd() * 2.0
+            r = rnd()
+            if r < 0.7 and cur[3]:
+                u, v = cur[3][int(rnd() * len(cur[3]))]
+                d = key[v] - key[u] + 1e-3 + rnd() * rnd() * 1.5
+                if r < 0.35:
+                    u, d = v, -d
             else:
-                key[u] = key[v] + 1e-3 + rnd() * rnd() * 2.0
-                stack = [u]
-                while stack:
-                    z = stack.pop()
-                    for j in succ[z]:
+                u = int(rnd() * n); d = (rnd() - 0.5) * 3.0 * rnd()
+            key[u] += d
+            ks = [u]
+            while d > 0 and ks:
+                nx = []
+                for z in ks:
+                    for j, _w in rev[z]:
                         if key[j] <= key[z]:
-                            key[j] = key[z] + 1e-6; stack.append(j)
-        s2, f2, w2 = run(legal(key))
-        sc = score(f2)
-        if sc < cur[0] + TEMP * (1.0 - it / ROUNDS) * rnd():
-            cur = (sc, s2, f2, w2)
-            if sc < best[0]:
-                best = cur
-    return legal(best[1]), best[1], max(best[2])
+                            key[j] = key[z] + 1e-6; nx.append(j)
+                ks = nx
+        c2 = fore(key)
+        if rnd() < TURN:
+            c2 = min(c2, turn(c2), key=lambda z: z[0])
+        if c2[0] < cur[0] + TEMP * (1.0 - it / ROUNDS) * rnd():
+            cur = c2
+            if c2[0] < best[0]:
+                best = c2
+    return legal(best[1]), best[1], best[2]
 
 
 ORDER = []

@@ -28,9 +28,9 @@ _sb("fl kc", 48, F16); _sb("rr d0c", 48, F32); _sb("lst", 48, U16); _sb("soff ao
 _sb("tb", TW, F32); _sb("srcb ssc", 224, BF); _sb("fh rc big", NV, F16); _sb("sur", 16, U16)
 _sb("nka eqa", 80, F16); _sb("asc", 16, F32); _sb("sm", 32, F32); _sb("junk", NV, F32)
 _sb("wo ho", NV, F32)
-_sb("jq", 256, F32); _sb("dq jb bf lf uf t1 t2 ba da", 128, F32); _sb("pi", 8, I32); _sb("g8i w8i", 144, I32)
-_sb("col", 32, F32); _sb("dg jm idw", 16, F32); _sb("jd db dc ds", 240, BF); _sb("wsc", NV, F32); _sb("addc", 8, F32)
-_sb("b16 i16 i2h i4k tri upp r0 r1 r2 r3 r4 g8 one", 128, F16); _sb("f16 w8", 144, F16); _sb("fb", 144, BF)
+_sb("jq", 256, F32); _sb("dq jb bf lf uf ba da", 128, F32); _sb("pi", 8, I32); _sb("g8i w8i", 144, I32)
+_sb("col", 32, F32); _sb("dg jm", 16, F32); _sb("idw", 26, F32); _sb("jd db dc ds", 240, BF); _sb("wsc", NV, F32); _sb("addc", 8, F32)
+_sb("b16 i16 i2h i4k tri upp r0 r1 r2 r3 g8 one", 128, F16); _sb("rf", 512, F32); _sb("f16 w8", 144, F16); _sb("fb", 144, BF)
 _sb("i2b bid", 128, BF); _sb("rw", 256, BF)
 for _i in range(8):
     SCRATCH["p%d" % _i] = ("psum", [128, 512], F32)
@@ -38,19 +38,19 @@ for _i in range(8):
 SEMAPHORES = (["ev", "es", "et", "eg", "loc"] + ["aw%d" % i for i in range(5)] + ["af%d" % i for i in range(4)]
               + ["dm%d" % i for i in range(12)])
 
-GA = [("v", 0, 32), ("s", 32, 64), ("v", 64, 80), ("s", 80, 144), ("s", 144, 192), ("v", 192, 208)]
+GA = [("v", 0, 32), ("s", 32, 64), ("v", 64, 96), ("s", 96, 144), ("s", 144, 192), ("s", 192, 208)]
 PRE = [(0, 64), (64, 144), (144, 208)]
 POST = [(0, 64), (64, 144), (144, 208)]
-NK16 = [(0, 128), (128, 208)]
-OFFQ = [("v", 0, 192)]
-ENG = {"tb": "s", "h16": "s", "ha": "v", "nkn": "sss", "nka": "v", "fa": "v", "d0": "vvvv", "soff": "sss",
-       "aoff": "v", "offa": "v", "nk16": "s", "lst": "v", "srcw": "v"}
-COST = {"cy": 0.00095, "pc": 0.00055, "ga": 1.56, "sc": 3.8, "hop": 0.10, "link": 2.0, "dif": 4.0, "nb": 6.5, "q": 9.0}
+NK16 = [(0, 208)]
+OFFQ = [("s", 0, 64), ("v", 64, 192)]
+ENG = {"tb": "s", "h16": "s", "ha": "s", "nkn": "sss", "nka": "v", "fa": "v", "d0": "vvvv", "soff": "sss",
+       "aoff": "v", "offa": "s", "nk16": "v", "srcw": "v", "cls": "s", "fh": "s", "sur": "s"}
+COST = {"fx": 0.0, "cy": 0.0009, "pc": 0.0005, "ga": 1.56, "sc": 3.8, "hop": 0.13, "link": 2.2, "dif": 4.5, "nb": 5.0, "q": 7.0}
 ROUNDS, TEMP, SEED, TURN, MARK = 35000, 0.4, 1, 0.3, 0.02
 
 
 def price(x, m):
-    return x["fx"] + m["cy"] * (x["cy"] + m["ga"] * x["ga"] + m["sc"] * x["sc"]) + m["pc"] * x["pe"]
+    return x["fx"] + (m["fx"] if x["k"] == "c" else 0.0) + m["cy"] * (x["cy"] + m["ga"] * x["ga"] + m["sc"] * x["sc"]) + m["pc"] * x["pe"]
 
 
 def build(g, core, T, topo):
@@ -168,7 +168,7 @@ def build(g, core, T, topo):
                 r = g.tensor.matmul(P(out), P(l), P(x), i == 0, i == len(pairs) - 1)
             return r
         ins = [z for pr in pairs for z in pr]
-        return node("t", f, [out], ins, {"fx": 0.05 + 0.005 * len(pairs), "pe": len(pairs) * max(64, out["n"])}, extra)
+        return node("t", f, [out], ins, {"fx": 0.05 + 0.005 * len(pairs), "pe": sum(4 if l["d"] == F32 else 1 for l, x in pairs) * max(64, out["n"])}, extra)
 
     def iota(out, pat, base, cm):
         if out["d"] == I32:
@@ -189,7 +189,7 @@ def build(g, core, T, topo):
         def f():
             for o_, i_ in pairs:
                 eng.dma_start(o_, i_).then_inc(T.sem[sem], 16)
-        return node(q, f, outs, ins, {"fx": 0.06 * len(pairs)}, extra, lat=lat, kind="d", sem=sem, cnt=16 * len(pairs))
+        chain("dma" + q, node(q, f, outs, ins, {"fx": 0.06 * len(pairs)}, extra, lat=lat, kind="d", sem=sem, cnt=16 * len(pairs)))
 
     sh = 16 * rank
 
@@ -214,8 +214,10 @@ def build(g, core, T, topo):
     PM, P16, E15, TC, SC, THR, RM, RB, AD, AD2, PM1, ID, R0 = range(13)
 
     def fill(name, lo, hi, v):
-        for x in range(lo, hi, 256):
-            act(a(name, x, min(hi, x + 256)), a("jq", 0, min(hi, x + 256) - x), bias=v, scale=0.0)
+        if SCRATCH[name][2] == F16:
+            ms(a(name, lo, hi), v)
+        else:
+            iota(a(name, lo, hi), [[0, hi - lo]], int(v), 0)
     iota(a("pi", 0, 1), [[0, 1]], 0, 1)
     iota(a("w8i", p=8), [[1, 144]], 16 * rank + 240, -16)
     iota(a("g8i", 0, 128, p=8), [[1, 8], [0, 16]], rank + 8, -1)
@@ -240,16 +242,16 @@ def build(g, core, T, topo):
     act(c(AD), c(E15), scale=-8192.0, bias=9216.0)
     act(c(AD2), c(E15), scale=-256.0, bias=256.0)
     act(c(PM1), c(PM), bias=1.0)
-    act(c(ID), c(PM), bias=float(SH))
-    act(c(R0), c(PM), bias=-(L + 1) / 2.0, scale=-1.0)
-    fill("big", 0, NV, 1000.0); fill("fh", L, NV, 0.0)
+    act(c(R0), c(PM), bias=-(L + 1.0), scale=-2.0)
+    act(c(ID), c(PM), bias=1.0, scale=2.0)
+    sg = 1.0 if ENG["fh"] == "s" else 0.0
+    fill("big", 0, NV, sg); fill("fh", L, NV, -sg)
     ts(a("bf"), a("jb"), c(P16), None, A.is_equal)
     act(a("b16"), a("bf"))
     asel(a("lf"), a("bf"), [[1, 128]], A.is_ge, 0.0, 0, -1)
     asel(a("uf"), a("bf"), [[-1, 128]], A.is_gt, 0.0, 0, 1)
-    for tmp, src, v, dst in (("t1", "lf", KC, "tri"), ("t2", "uf", 1 - KC, "upp")):
-        asel(a(tmp), a(src), [[1, 128]], A.not_equal, float(v), 0, -1)
-        act(a(dst), a(tmp))
+    for src, v, dst in (("lf", KC, "tri"), ("uf", 1 - KC, "upp")):
+        asel(a(dst), a(src), [[1, 128]], A.not_equal, float(v), 0, -1)
     ts(a("fb"), a("jq", 0, 144), c(P16), 16.0, A.subtract, A.is_equal)
     act(a("f16"), a("fb"))
     ts(a("rw", 0, 128), a("dq"), 0.0, None, A.is_equal)
@@ -259,37 +261,40 @@ def build(g, core, T, topo):
     ts(a("ba"), a("dq"), c(TC), c(SC), A.is_equal, A.mult)
     asel(a("bid"), a("ba"), [[1, 128]], A.not_equal, 0.5, 0, -1)
     ts(a("dg"), a("jq", 0, 16), c(PM), None, A.is_equal)
-    for p in range(5):
+    for p in range(4):
         act(a("r%d" % p), a("bf"), scale=a("dg", p, p + 1))
+        act(a("rf", 128 * p, 128 * p + 128), a("bf"), scale=a("dg", p + 1, p + 2))
     ts(a("db"), a("jd"), c(PM1), -256.0, A.is_equal, A.mult)
     ts(a("dc"), a("jd"), c(PM), 2048.0, A.is_equal, A.mult)
     tt(a("ds"), a("dc"), a("db"), A.add)
     act(a("da"), a("ds", 0, 128), scale=32.0)
     act(a("addc"), a("jq", 0, 8), scale=0.0, bias=c(AD))
-    act(a("idw"), a("jm"), bias=c(ID))
+    ms(a("idw", 12, 14), 0.0)
+    act(a("idw", 0, 12), a("jm", 0, 12), bias=c(PM)); act(a("idw", 14, 26), a("jm", 0, 12), bias=c(PM))
     act(a("tb", 0, L), a("jq", O, O + L), AF.Silu if ENG["tb"] == "s" else AF.Identity)
     ms(a("tb", MU, SW), 1.0); ms(a("tb", MU + 1, MU + 2), 2.0); ms(a("tb", MU + 2, MU + 3), 0.5)
     fill("tb", SW, CP, 0.0)
     fill("one", 0, 128, 1.0)
-    ms(a("kc"), 0.0); ms(a("kc", 12, 13), float(SH)); ms(a("kc", 14, 28, 13), float(SW)); ms(a("kc", 28, 40), float(SH + MU))
-    ms(a("d0c"), 1.0); ms(a("d0c", 14, 15), 0.0); ms(a("d0c", 28, 40), 0.0)
+    ms(a("kc"), 0.0); ms(a("kc", 0, 1), float(-SH)); ms(a("kc", 12, 13), float(SH)); ms(a("kc", 14, 15), float(SW - SH)); ms(a("kc", 27, 28), float(SW))
+    ms(a("d0c"), 1.0); ms(a("d0c", 14, 15), 0.0)
     ms(a("fl", 0, 1), 0.0)
     for x in (L, NV + 16 + L):
-        fill("mm", x, x + 16, 1.0); fill("mm", x + 16, x + 32, 0.0)
+        fill("mm", x, x + 32, 0.0); fill("mm", x, x + 16, 1.0)
     for x in range(0, 3344, 836):
         ms(a("d0", x, x + 836), 60000.0)
     fill("xq", 0, 16, float(NO))
     fill("qw", 0, 16, 0.0)
     fill("ub", 0, O, 0.0); fill("ub", NV, NV + O, 0.0)
-    fill("w1", 0, 240, 0.0); fill("hw", 0, 240, 0.0); fill("hf", 0, 240, -1.0); fill("nkm", 0, 240, -4096.0)
+    for nm, v in (("w1", 0.0), ("hw", 0.0), ("hf", -1.0), ("nkm", -4096.0)):
+        fill(nm, 0, O, v); fill(nm, NV, 240, v)
     fill("wo", 0, O, 0.0); fill("ho", 0, O, 0.0)
     E = lambda k: a("f16", 16 - k, 144 - k)
     EB = lambda k: a("fb", 16 - k, 144 - k)
 
-    ts(a("ush", p=8), a("usi", p=8), -8.0, None, A.mult)
-    ts(a("coh", p=8), a("coi", p=8), -1.0, 1.0, A.mult, A.add)
     for t in range(ST):
         pb = "p%d" % (t % 2)
+        ts(a("ush", t * L, t * L + L, p=8), a("usi", t * L, t * L + L, p=8), -8.0, None, A.mult)
+        ts(a("coh", t * L, t * L + L, p=8), a("coi", t * L, t * L + L, p=8), -1.0, 1.0, A.mult, A.add)
         mm(a(pb, 0, L), [(a("g8", p=8), a("ush", t * L, t * L + L, p=8))])
         mm(a(pb, L, 2 * L), [(a("g8", p=8), a("coh", t * L, t * L + L, p=8))])
         act(a("ub", O + t * NV, O + t * NV + L), a(pb, 0, L))
@@ -311,7 +316,8 @@ def build(g, core, T, topo):
     s = lambda j: a("sm", j, j + 1)
     PD, YY, NVA, SG, FA, NH, NC = range(7)
     act(a("junk", 0, L), a("p3", 0, L), AF.Sign, bias=1024.5, accum=s(NVA))
-    act(s(PD), s(NVA), bias=L / 2.0, scale=-0.5)
+    act(s(YY), c(R0), scale=-1.0)
+    act(s(PD), s(NVA), bias=s(YY), scale=-1.0)
 
     peers = [T.cores[(rank + d) % n_r] for d in range(1, n_r)]
     nxt = T.cores[(rank + DR) % n_r]
@@ -329,16 +335,17 @@ def build(g, core, T, topo):
         if t > 0:
             k = t + 1
             lin(ENG["ha"], a("h16", L, NV), a(wv, NV, 224), extra=[arr_w])
-            for p in range(k - 1, -1, -1):
-                mm(a("p7", 256 + 16 * p, 272 + 16 * p), [(a("r%d" % p), a("h16", L, NV))])
+            mm(a("p7", 256 + 16 * t, 272 + 16 * t), [(a("rf", 128 * t - 128, 128 * t), a(wv, NV, 224))], extra=[arr_w])
             scan(a("asc"), a("da", 0, 16), a("p7", 256 + 16 * t, 272 + 16 * t), 0.0, A.add, A.min)
+            for p in range(t):
+                mm(a("p7", 256 + 16 * p, 272 + 16 * p), [(a("r%d" % p), a("h16", L, NV))])
             off(ENG["aoff"], a("aoff", 0, k), a("addc", 0, k), a("asc", 15, 16))
             lin(ENG["nka"], a("nka", 0, 16 * k), ind(a("nbs"), a("aoff", 0, k)), bias=-1024.0)
             tt(a("eqa", 0, 16 * k), a("nka", 0, 16 * k), a("p7", 256, 256 + 16 * k), A.is_equal)
             mm(a("p7", 352, 368), [(a("i16"), a("nka", 0, 16))] + [(a("i4k"), a("eqa", 16 * p, 16 * p + 16)) for p in range(k)])
             off(ENG["offa"], a("offq", L, NV), a("p7", 352, 368), 1040.0)
             act(a("junk", 0, 16), a(wv, L, NV), AF.Sign, accum=s(NVA), extra=[arr_w])
-            act(s(PD), s(NVA), AF.Relu, bias=s(YY), scale=-1.0)
+            act(s(PD), s(NVA), bias=s(YY), scale=-2.0)
             prs = [(a("rw", 0, 128), a("dif", 8 * t - 8, 8 * t - 7))]
             for d in range(1, n_r):
                 r2 = 8 * t - 8 + (rank + d) % n_r
@@ -389,12 +396,13 @@ def build(g, core, T, topo):
             tt(yy, pb, a("nk16", lo, hi), A.mult)
             if not last:
                 mm(a(bank, 256, 256 + n), [(a("b16"), yy)])
-            mm(a(bank, 384, 384 + n), [(a("i16"), a("h16", lo, hi)), (E(t + 1), yy)])
+            hp = a(bank, 384, 384 + n) if last else a("p7", lo, hi)
+            mm(hp, [(a("i16"), a("h16", lo, hi)), (E(t + 1), yy)])
             if last:
-                act(a(hw, O + lo, O + hi), a(bank, 384, 384 + n), bias=c(RB), scale=c(RM))
+                act(a(hw, O + lo, O + hi), hp, bias=c(RB), scale=c(RM))
                 continue
+            act(a(hw, O + lo, O + hi), hp)
             scan(a("wsc", lo, hi), a("da", 0, n), a(bank, 256, 256 + n), 0.0, A.add, A.min)
-            act(a(hw, O + lo, O + hi), a(bank, 384, 384 + n))
             so = a("soff", 8 * ci, 8 * ci + n // 16)
             off(ENG["soff"][ci], so, a("wsc", lo + 15, hi, 16), c(AD))
             nk = a("nkn", lo, hi)
@@ -415,21 +423,24 @@ def build(g, core, T, topo):
         ts(a("mm", 448, 640), w1, a(lh, t, t + 1), None, A.is_lt)
         mm(a("p5", 304, 496), [(a("b16"), a("mm", 0, L))])
         mm(a("p5", 0, L), [(a("b16"), a("mm", 224, 224 + L))])
-        ts(a("fh", 0, L), a("p5", 304, 496), 9.5, None, A.is_gt)
+        if ENG["fh"] == "s":
+            act(a("fh", 0, L), a("p5", 304, 496), AF.Sign, bias=-9.5)
+        else:
+            ts(a("fh", 0, L), a("p5", 304, 496), 9.5, 2.0, A.is_gt, A.mult)
         act(a("junk", 0, L), a("p5", 0, L), AF.Sign, bias=-9.5, accum=s(NH))
-        scan(a("rc"), a("fh"), a("big"), c(R0), A.add, A.min)
-        act(a("junk"), a("rc"), AF.Sign, bias=s(NH), scale=-2.0, accum=s(NC))
+        scan(a("rc"), a("fh"), a("big"), c(R0), A.add, A.add)
+        act(a("junk"), a("rc"), AF.Sign, bias=s(NH), scale=-1.0, accum=s(NC))
         sur = a("sur", 2 * t, 2 * t + 1)
-        ts(sur, s(NC), 0.5, float(NV // 2 + O), A.mult, A.add)
+        lin(ENG["sur"], sur, s(NC), 0.5, float(NV // 2 + O))
         mm(a("p6", 0, 40), [(E(r), a("mm", r, 640, 16)) for r in range(16)])
         ts(a("fl", 1, 41), a("p6", 0, 40), 9.5, None, A.is_gt)
         one = a("one", p=1)
         mm(a("p6", 64, 92), [(one, a("kc", 0, 28, p=1)), (a("tri"), a("fl", 1, 29)), (a("upp"), a("fl", 0, 28))])
-        mm(a("p6", 92, 104), [(one, a("kc", 28, 40, p=1)), (a("i16"), a("fl", 29, 41)), (a("i16"), a("fl", 15, 27)), (a("i2h"), a("fl", 1, 13))])
-        scan(a("rr", 0, 40), a("d0c", 0, 40), a("p6", 64, 104), 0.0, A.mult, A.add)
-        tt(a("rr", 14, 26), a("rr", 14, 26), a("idw", 0, 12), A.max)
-        tt(a("rr", 0, 12), a("rr", 0, 12), a("rr", 14, 26), A.max)
-        off(ENG["lst"], a("lst", 0, 40), a("rr", 0, 40), float(-SH))
+        scan(a("rr", 0, 28), a("d0c", 0, 28), a("p6", 64, 92), 0.0, A.mult, A.add)
+        mm(a("p6", 92, 104), [(a("i16"), a("fl", 29, 41)), (a("i16"), a("fl", 15, 27)), (a("i2h"), a("fl", 1, 13))])
+        off(ENG["cls"], a("lst", 28, 40), a("p6", 92, 104), float(MU))
+        tt(a("lst", 0, 26), a("rr", 0, 26), a("idw"), A.max)
+        tt(a("lst", 0, 12), a("lst", 0, 12), a("rr", 14, 26), A.max)
         if ENG["tb"] == "s":
             act(ind(a("tb", SW, TW), a("lst", 0, 12)), a("tb", 0, L), AF.Silu)
         else:
@@ -471,9 +482,9 @@ def build(g, core, T, topo):
             lin(ENG["h16"], a("h16", 0, L), ind(a(hw), src))
             uo2 = uo + NV
             act(a("ub", uo2 + L, uo2 + NV), ind(a("ub", uo2 - O, uo2 + L), dst))
-            act(s(YY), a("rr", 13, 14), bias=a("rr", 27, 28), scale=-1.0)
+            act(s(YY), a("rc", NV - 1, NV), bias=s(NH), scale=-1.0)
             dif = a("dif", 8 * t, 8 * t + 1)
-            act(dif, s(YY), bias=s(PD), scale=-1.0)
+            ts(dif, s(PD), c(ID), s(YY), A.max, A.subtract)
             m7 = msk
             for q in peers:
                 m7 = m7 & topo.mask(core, q)

from concourse.bass import DstId, RemoteDMATransfer
from concourse.mybir import AluOpType, ActivationFunctionType

NS, L, NV, ST, DR = 3072, 192, 208, 5, 3
O, ZC = 16, 224
MU, SW, CP, HL, TW = 192, 208, 400, 608, 816
KC, SH = 608, 416
NO = 255 * 128
F32, F16, BF, I32, U16 = "float32", "float16", "bfloat16", "int32", "uint16"

SCRATCH = {}


def _sb(names, cols, dtype):
    for n in names.split():
        SCRATCH[n] = ("sbuf", [128, cols], dtype)


_sb("nbs", NS, I32); _sb("qw", NS + 16, BF); _sb("xq dd", 3344, BF); _sb("d0", 3344, F16)
_sb("s0i", L, I32); _sb("usi coi", 960, I32); _sb("s0h dm", L, F16); _sb("ush coh", 960, F16)
_sb("lor hir", 8, F32); _sb("lh0 lh1", 16, F32)
_sb("ub", 16 + ST * NV, BF); _sb("nco", 960, BF)
_sb("offq", NV, U16); _sb("nk16 h16 yy nkn", NV, F16); _sb("eqs", 5 * NV, F16); _sb("ge", NV, BF)
_sb("wv0 wv1 wv2 wv3 wv4 wv5 w1 hw hf nkm", 240, F32)
_sb("snd", 160, F32); _sb("cnt dif", 32, BF)
_sb("nt", NV, F32); _sb("ti", NV, I32); _sb("mm", 640, F16); _sb("mu", L, F32)
_sb("fl kc", 48, F16); _sb("rr d0c", 48, F32); _sb("lst", 48, U16); _sb("soff aoff srcw0 srcw1", 32, U16)
_sb("tb", TW, F32); _sb("srcb ssc", 224, BF); _sb("fh rc big", NV, F16); _sb("sur", 16, U16)
_sb("nka eqa", 80, F16); _sb("asc", 16, F32); _sb("sm", 32, F32); _sb("junk", NV, F32)
_sb("wo ho", NV, F32)
_sb("jq", 256, F32); _sb("dq jb bf lf uf ba da", 128, F32); _sb("pi", 8, I32); _sb("g8i w8i", 144, I32)
_sb("col", 32, F32); _sb("dg jm", 16, F32); _sb("idw", 26, F32); _sb("jd db dc ds", 240, BF); _sb("wsc", NV, F32); _sb("addc", 8, F32)
_sb("b16 i16 i2h i4k tri upp r0 r1 r2 r3 g8 one", 128, F16); _sb("rf", 512, F32); _sb("f16 w8", 144, F16); _sb("fb", 144, BF)
_sb("i2b bid", 128, BF); _sb("rw", 256, BF)
for _i in range(8):
    SCRATCH["p%d" % _i] = ("psum", [128, 512], F32)

SEMAPHORES = (["ev", "es", "et", "eg", "loc"] + ["aw%d" % i for i in range(5)] + ["af%d" % i for i in range(4)]
              + ["dm%d" % i for i in range(12)])

GA = [("v", 0, 32), ("s", 32, 64), ("v", 64, 96), ("s", 96, 144), ("s", 144, 192), ("s", 192, 208)]
PRE = [(0, 64), (64, 144), (144, 208)]
POST = [(0, 64), (64, 144), (144, 208)]
NK16 = [(0, 208)]
OFFQ = [("s", 0, 64), ("v", 64, 192)]
ENG = {"tb": "s", "h16": "s", "ha": "s", "nkn": "sss", "nka": "v", "fa": "v", "d0": "vvvv", "soff": "sss",
       "aoff": "v", "offa": "s", "nk16": "v", "srcw": "v", "cls": "s", "fh": "s", "sur": "s"}
COST = {"fx": 0.0, "cy": 0.0009, "pc": 0.0005, "ga": 1.56, "sc": 3.8, "hop": 0.13, "link": 2.2, "dif": 4.5, "nb": 5.0, "q": 7.0}
ROUNDS, TEMP, SEED, TURN, MARK = 35000, 0.4, 1, 0.3, 0.02


def price(x, m):
    return x["fx"] + (m["fx"] if x["k"] == "c" else 0.0) + m["cy"] * (x["cy"] + m["ga"] * x["ga"] + m["sc"] * x["sc"]) + m["pc"] * x["pe"]


def build(g, core, T, topo):
    rank = T.rank_of(core)
    n_r = len(T.cores)
    A = AluOpType
    AF = ActivationFunctionType
    nodes = []
    acc = {}

    def a(name, lo=0, hi=None, step=1, p=128):
        if hi is None:
            hi = SCRATCH[name][1][1]
        v = T[name][0:p, lo:hi] if step == 1 else T[name][0:p, lo:hi:step]
        return {"ap": v, "r": [(name, lo, hi)], "n": len(range(lo, hi, step)), "m": SCRATCH[name][0], "d": SCRATCH[name][2], "ind": 0}

    def ind(win, off):
        return {"ap": win["ap"].indirect(off["ap"]), "r": win["r"], "o": off["r"], "n": 16 * off["n"], "m": "sbuf", "d": win["d"], "ind": 1}

    def node(eng, fn, outs, ins, cost, extra=(), lat=None, kind="c", sem=None, cnt=0):
        k = len(nodes)
        deps = set(extra)
        wr = []; rd = []
        for x in outs:
            wr += x["r"]; rd += x.get("o", [])
        for x in ins:
            if isinstance(x, dict):
                rd += x["r"] + x.get("o", [])
        for regs, w in ((wr, True), (rd, False)):
            for (nm, lo, hi) in regs:
                ps = SCRATCH[nm][0] == "psum"
                for (j, e2, l2, h2, w2) in acc.setdefault(nm, []):
                    if j != k and (((w or w2) and lo < h2 and l2 < hi) or (ps and e2 != eng)):
                        deps.add(j)
                if w and not ps:
                    acc[nm] = [z for z in acc[nm] if not (lo <= z[2] and z[3] <= hi)]
                acc[nm].append((k, eng, lo, hi, w))
        x = {"fx": 0.0, "cy": 0, "ga": 0, "sc": 0, "pe": 0}
        x.update(cost)
        x.update({"e": eng, "f": fn, "deps": sorted(deps), "after": [], "lat": lat, "k": kind, "sem": sem, "cnt": cnt, "nm": (wr[:1], rd[:2])})
        x["t"] = step[0]
        nodes.append(x)
        return k

    step = [None]

    tail = {}

    def chain(key, k):
        if key in tail:
            nodes[k]["after"].append(tail[key])
        tail[key] = k

    def P(x):
        return x["ap"] if isinstance(x, dict) else x

    def vc(out, ins, two=False, fx=0.05, fast=True):
        xs = [out] + [x for x in ins if isinstance(x, dict) and x["n"] > 1]
        n = max(x["n"] for x in xs)
        if out["ind"]:
            return {"fx": fx, "sc": n}
        if any(x["ind"] for x in xs):
            return {"fx": fx, "ga": n}
        c = 0.5 if fast and all(x["d"] in (F16, BF, U16) for x in xs) else 1.0
        if two:
            c = 2.0 if all(x["m"] == "sbuf" for x in ins) else 1.0
        return {"fx": fx, "cy": max(64, n * c)}

    def ts(out, i0, s1, s2, op0, op1=None, extra=()):
        if op1 is None:
            f = lambda: g.vector.tensor_scalar(P(out), P(i0), P(s1), None, op0)
        else:
            f = lambda: g.vector.tensor_scalar(P(out), P(i0), P(s1), P(s2), op0, op1)
        return node("v", f, [out], [i0, s1, s2], vc(out, [i0]), extra)

    def tt(out, i0, i1, op, extra=()):
        return node("v", lambda: g.vector.tensor_tensor(P(out), P(i0), P(i1), op), [out], [i0, i1], vc(out, [i0, i1], True), extra)

    def cp(out, i0, extra=()):
        return node("v", lambda: g.vector.tensor_copy(P(out), P(i0)), [out], [i0], vc(out, [i0]), extra)

    def ms(out, c):
        return node("v", lambda: g.vector.memset(P(out), c), [out], [], vc(out, []))

    def scan(out, d0, d1, init, op0, op1):
        return node("v", lambda: g.vector.tensor_tensor_scan(P(out), P(d0), P(d1), P(init), op0, op1), [out], [d0, d1, init], vc(out, [d0, d1]))

    def act(out, i0, func=None, bias=0.0, scale=1.0, accum=None, extra=()):
        func = AF.Identity if func is None else func
        cost = vc(out, [i0], fx=0.065 if accum is None else 0.085, fast=False)
        if out["ind"]:
            return node("s", lambda: g.scalar.activation(P(out), P(i0), func), [out], [i0], cost, extra)
        if accum is None:
            f = lambda: g.scalar.activation(P(out), P(i0), func, bias=P(bias), scale=P(scale))
            return node("s", f, [out], [i0, bias, scale], cost, extra)
        f = lambda: g.scalar.activation(P(out), P(i0), func, bias=P(bias), scale=P(scale), accum_out=P(accum))
        return node("s", f, [out, accum], [i0, bias, scale], cost, extra)

    def lin(e, out, i0, scale=1.0, bias=0.0, extra=()):
        if e == "s":
            return act(out, i0, bias=bias, scale=scale, extra=extra)
        if scale == 1.0 and bias == 0.0:
            return cp(out, i0, extra)
        return ts(out, i0, scale, bias, A.mult, A.add, extra)

    def off(e, out, i0, bias):
        if e == "s":
            return act(out, i0, AF.Relu, bias=bias)
        return ts(out, i0, bias, None, A.add)

    def mm(out, pairs, extra=()):
        def f():
            r = None
            for i, (l, x) in enumerate(pairs):
                r = g.tensor.matmul(P(out), P(l), P(x), i == 0, i == len(pairs) - 1)
            return r
        ins = [z for pr in pairs for z in pr]
        return node("t", f, [out], ins, {"fx": 0.05 + 0.005 * len(pairs), "pe": sum(4 if l["d"] == F32 else 1 for l, x in pairs) * max(64, out["n"])}, extra)

    def iota(out, pat, base, cm):
        if out["d"] == I32:
            f = lambda: g.iota(P(out), pat, base, cm)
        else:
            f = lambda: g.iota(P(out), pat, base, cm, allow_small_or_imprecise_dtypes=True)
        return node("g", f, [out], [], {"fx": 0.13, "cy": 2 * out["n"]})

    def asel(out, i0, pat, op, fill, base, cm):
        return node("g", lambda: g.affine_select(P(out), P(i0), pat, op, fill, base, cm), [out], [i0], {"fx": 0.17, "cy": 2 * out["n"]})

    ndma = [0]

    def dma(q, pairs, outs, ins, lat, extra=()):
        sem = "dm%d" % ndma[0]; ndma[0] += 1
        eng = g.sync if q == "y" else g.scalar

        def f():
            for o_, i_ in pairs:
                eng.dma_start(o_, i_).then_inc(T.sem[sem], 16)
        chain("dma" + q, node(q, f, outs, ins, {"fx": 0.06 * len(pairs)}, extra, lat=lat, kind="d", sem=sem, cnt=16 * len(pairs)))

    sh = 16 * rank

    def rot_in(name, src, lo, hi):
        if sh == 0:
            return [(T[name][:, lo:hi], src[:, :])]
        return [(T[name][0:128 - sh, lo:hi], src[sh:128, :]), (T[name][128 - sh:128, lo:hi], src[0:sh, :])]

    def rot_out(dst, name, lo, hi):
        if sh == 0:
            return [(dst[:, :], T[name][:, lo:hi])]
        return [(dst[sh:128, :], T[name][0:128 - sh, lo:hi]), (dst[0:sh, :], T[name][128 - sh:128, lo:hi])]

    dma("s", [(T.s0i[0:8, :], T.s0[:, :])], [a("s0i")], [], 2.0)
    dma("s", [(T.usi[0:8, :], T.us[:, :]), (T.coi[0:8, :], T.coin[:, :])], [a("usi"), a("coi")], [], 2.5)
    dma("y", rot_in("nbs", T.nb, 0, NS), [a("nbs")], [], "nb")
    dma("y", rot_in("qw", T.qs, 16, 16 + NS), [a("qw", 16, 16 + NS)], [], "q")
    dma("y", rot_in("wv0", T.w0, 0, L), [a("wv0", 0, L)], [], "q")
    dma("y", rot_in("lor", T.lo, 0, ST) + rot_in("hir", T.hi, 0, ST), [a("lor"), a("hir")], [], "q")

    c = lambda j: a("col", j, j + 1)
    PM, P16, E15, TC, SC, THR, RM, RB, AD, AD2, PM1, ID, R0 = range(13)

    def fill(name, lo, hi, v):
        if SCRATCH[name][2] == F16:
            ms(a(name, lo, hi), v)
        else:
            iota(a(name, lo, hi), [[0, hi - lo]], int(v), 0)
    iota(a("pi", 0, 1), [[0, 1]], 0, 1)
    iota(a("w8i", p=8), [[1, 144]], 16 * rank + 240, -16)
    iota(a("g8i", 0, 128, p=8), [[1, 8], [0, 16]], rank + 8, -1)
    iota(a("jq"), [[1, 256]], 0, 0)
    iota(a("dq"), [[1, 128]], 0, -1)
    iota(a("jb"), [[16, 8], [0, 16]], 0, 0)
    iota(a("jm"), [[16, 16]], 0, 0)
    iota(a("jd"), [[0, 15], [1, 16]], 0, 0)
    ts(a("g8i", 0, 128, p=8), a("g8i", 0, 128, p=8), 7, None, A.bitwise_and)
    ts(a("g8", p=8), a("g8i", 0, 128, p=8), 0.0, None, A.is_equal)
    ts(a("w8i", p=8), a("w8i", p=8), 127, None, A.bitwise_and)
    ts(a("w8", p=8), a("w8i", p=8), 0.0, None, A.is_equal)
    ts(a("pi", 1, 2), a("pi", 0, 1), 15, None, A.bitwise_and)
    cp(c(PM), a("pi", 1, 2))
    ts(c(P16), a("pi", 0, 1), c(PM), None, A.subtract)
    ts(c(E15), c(PM), 15.0, None, A.is_equal)
    act(c(TC), c(E15), scale=-16.0, bias=1.0)
    act(c(SC), c(E15), bias=-0.5)
    act(c(THR), c(E15), scale=16.0 * NO + 1280.0, bias=-16.0 * NO - 1216.0)
    ts(c(RM), c(PM), 5.5, None, A.is_lt)
    act(c(RB), c(RM), scale=1025.0, bias=-1.0)
    act(c(AD), c(E15), scale=-8192.0, bias=9216.0)
    act(c(AD2), c(E15), scale=-256.0, bias=256.0)
    act(c(PM1), c(PM), bias=1.0)
    act(c(R0), c(PM), bias=-(L + 1.0), scale=-2.0)
    act(c(ID), c(PM), bias=1.0, scale=2.0)
    sg = 1.0 if ENG["fh"] == "s" else 0.0
    fill("big", 0, NV, sg); fill("fh", L, NV, -sg)
    ts(a("bf"), a("jb"), c(P16), None, A.is_equal)
    act(a("b16"), a("bf"))
    asel(a("lf"), a("bf"), [[1, 128]], A.is_ge, 0.0, 0, -1)
    asel(a("uf"), a("bf"), [[-1, 128]], A.is_gt, 0.0, 0, 1)
    for src, v, dst in (("lf", KC, "tri"), ("uf", 1 - KC, "upp")):
        asel(a(dst), a(src), [[1, 128]], A.not_equal, float(v), 0, -1)
    ts(a("fb"), a("jq", 0, 144), c(P16), 16.0, A.subtract, A.is_equal)
    act(a("f16"), a("fb"))
    ts(a("rw", 0, 128), a("dq"), 0.0, None, A.is_equal)
    act(a("rw", 128, 256), a("rw", 0, 128))
    for nm, v in (("i16", 1.0), ("i2h", 2.0), ("i4k", -4096.0), ("i2b", 2.0 ** -6)):
        act(a(nm), a("rw", 0, 128), scale=v)
    ts(a("ba"), a("dq"), c(TC), c(SC), A.is_equal, A.mult)
    asel(a("bid"), a("ba"), [[1, 128]], A.not_equal, 0.5, 0, -1)
    ts(a("dg"), a("jq", 0, 16), c(PM), None, A.is_equal)
    for p in range(4):
        act(a("r%d" % p), a("bf"), scale=a("dg", p, p + 1))
        act(a("rf", 128 * p, 128 * p + 128), a("bf"), scale=a("dg", p + 1, p + 2))
    ts(a("db"), a("jd"), c(PM1), -256.0, A.is_equal, A.mult)
    ts(a("dc"), a("jd"), c(PM), 2048.0, A.is_equal, A.mult)
    tt(a("ds"), a("dc"), a("db"), A.add)
    act(a("da"), a("ds", 0, 128), scale=32.0)
    act(a("addc"), a("jq", 0, 8), scale=0.0, bias=c(AD))
    ms(a("idw", 12, 14), 0.0)
    act(a("idw", 0, 12), a("jm", 0, 12), bias=c(PM)); act(a("idw", 14, 26), a("jm", 0, 12), bias=c(PM))
    act(a("tb", 0, L), a("jq", O, O + L), AF.Silu if ENG["tb"] == "s" else AF.Identity)
    ms(a("tb", MU, SW), 1.0); ms(a("tb", MU + 1, MU + 2), 2.0); ms(a("tb", MU + 2, MU + 3), 0.5)
    fill("tb", SW, CP, 0.0)
    fill("one", 0, 128, 1.0)
    ms(a("kc"), 0.0); ms(a("kc", 0, 1), float(-SH)); ms(a("kc", 12, 13), float(SH)); ms(a("kc", 14, 15), float(SW - SH)); ms(a("kc", 27, 28), float(SW))
    ms(a("d0c"), 1.0); ms(a("d0c", 14, 15), 0.0)
    ms(a("fl", 0, 1), 0.0)
    for x in (L, NV + 16 + L):
        fill("mm", x, x + 32, 0.0); fill("mm", x, x + 16, 1.0)
    for x in range(0, 3344, 836):
        ms(a("d0", x, x + 836), 60000.0)
    fill("xq", 0, 16, float(NO))
    fill("qw", 0, 16, 0.0)
    fill("ub", 0, O, 0.0); fill("ub", NV, NV + O, 0.0)
    for nm, v in (("w1", 0.0), ("hw", 0.0), ("hf", -1.0), ("nkm", -4096.0)):
        fill(nm, 0, O, v); fill(nm, NV, 240, v)
    fill("wo", 0, O, 0.0); fill("ho", 0, O, 0.0)
    E = lambda k: a("f16", 16 - k, 144 - k)
    EB = lambda k: a("fb", 16 - k, 144 - k)

    for t in range(ST):
        pb = "p%d" % (t % 2)
        ts(a("ush", t * L, t * L + L, p=8), a("usi", t * L, t * L + L, p=8), -8.0, None, A.mult)
        ts(a("coh", t * L, t * L + L, p=8), a("coi", t * L, t * L + L, p=8), -1.0, 1.0, A.mult, A.add)
        mm(a(pb, 0, L), [(a("g8", p=8), a("ush", t * L, t * L + L, p=8))])
        mm(a(pb, L, 2 * L), [(a("g8", p=8), a("coh", t * L, t * L + L, p=8))])
        act(a("ub", O + t * NV, O + t * NV + L), a(pb, 0, L))
        act(a("nco", t * L, t * L + L), a(pb, L, 2 * L))
    fill("lh0", 0, 16, 0.0)
    act(a("lh0", 0, ST), a("lor", 0, ST)); act(a("lh0", 8, 8 + ST), a("hir", 0, ST))

    ts(a("s0h", p=8), a("s0i", p=8), -1024.0, None, A.add)
    mm(a("p6", 0, 12), [(a("w8", 16 - r, 144 - r, p=8), a("s0h", r, L, 16, p=8)) for r in range(16)])
    ts(a("soff", 0, 12), a("p6", 0, 12), 1024.0, None, A.add)
    mm(a("p3", 0, L), [(a("g8", p=8), a("s0h", p=8))])
    mm(a("p4", 0, L), [(a("w8", 16, 144, p=8), a("s0h", p=8))])
    ts(a("dm"), a("p3", 0, L), -1024.5, None, A.is_lt)
    ts(a("nkn", 0, L), ind(a("nbs"), a("soff", 0, 12)), -1024.0, None, A.add)
    tt(a("eqs", 0, L), a("nkn", 0, L), a("p3", 0, L), A.is_equal)
    mm(a("p7", 0, L), [(a("i4k"), a("dm")), (a("i16"), a("nkn", 0, L)), (a("i4k"), a("eqs", 0, L))])
    off("v", a("offq", 0, L), a("p7", 0, L), 1040.0)
    act(a("h16", 0, L), a("p4", 0, L))
    s = lambda j: a("sm", j, j + 1)
    PD, YY, NVA, SG, FA, NH, NC = range(7)
    act(a("junk", 0, L), a("p3", 0, L), AF.Sign, bias=1024.5, accum=s(NVA))
    act(s(YY), c(R0), scale=-1.0)
    act(s(PD), s(NVA), bias=s(YY), scale=-1.0)

    peers = [T.cores[(rank + d) % n_r] for d in range(1, n_r)]
    nxt = T.cores[(rank + DR) % n_r]
    nloc = [0]
    arr_w = None; arr_f = None
    lh = "lh0"
    for t in range(ST):
        step[0] = t
        nv = L if t == 0 else NV
        last = t == ST - 1
        wv = "wv%d" % t
        uo = O + t * NV
        hw = "hf" if last else "hw"
        cut = lambda ch: [z[:-1] + (min(z[-1], nv),) for z in ch if z[-2] < nv]
        if t > 0:
            k = t + 1
            lin(ENG["ha"], a("h16", L, NV), a(wv, NV, 224), extra=[arr_w])
            mm(a("p7", 256 + 16 * t, 272 + 16 * t), [(a("rf", 128 * t - 128, 128 * t), a(wv, NV, 224))], extra=[arr_w])
            scan(a("asc"), a("da", 0, 16), a("p7", 256 + 16 * t, 272 + 16 * t), 0.0, A.add, A.min)
            for p in range(t):
                mm(a("p7", 256 + 16 * p, 272 + 16 * p), [(a("r%d" % p), a("h16", L, NV))])
            off(ENG["aoff"], a("aoff", 0, k), a("addc", 0, k), a("asc", 15, 16))
            lin(ENG["nka"], a("nka", 0, 16 * k), ind(a("nbs"), a("aoff", 0, k)), bias=-1024.0)
            tt(a("eqa", 0, 16 * k), a("nka", 0, 16 * k), a("p7", 256, 256 + 16 * k), A.is_equal)
            mm(a("p7", 352, 368), [(a("i16"), a("nka", 0, 16))] + [(a("i4k"), a("eqa", 16 * p, 16 * p + 16)) for p in range(k)])
            off(ENG["offa"], a("offq", L, NV), a("p7", 352, 368), 1040.0)
            act(a("junk", 0, 16), a(wv, L, NV), AF.Sign, accum=s(NVA), extra=[arr_w])
            act(s(PD), s(NVA), bias=s(YY), scale=-2.0)
            prs = [(a("rw", 0, 128), a("dif", 8 * t - 8, 8 * t - 7))]
            for d in range(1, n_r):
                r2 = 8 * t - 8 + (rank + d) % n_r
                prs.append((a("rw", 128 - 16 * d, 256 - 16 * d), a("cnt", r2, r2 + 1)))
            mm(a("p5", 300, 301), prs, extra=[arr_f])
            if ENG["fa"] == "s":
                act(s(SG), a("p5", 300, 301), AF.Sign, bias=-0.5)
                act(s(FA), s(SG), bias=1.5, scale=0.5)
            else:
                ts(s(FA), a("p5", 300, 301), 0.5, 1.0, A.is_gt, A.add)
            lh2 = "lh%d" % (t % 2)
            act(a(lh2), a(lh), scale=s(FA))
            lh = lh2
        for (lo, hi) in cut(NK16):
            lin(ENG["nk16"], a("nk16", lo, hi), a("offq", lo, hi), bias=-1040.0)
        act(a("p5", 0, L), a("nco", t * L, t * L + L), bias=2.0 ** -120, scale=a(lh, t, t + 1))
        iota(a("tb", CP, TW), [[-ZC, 2], [0, 13], [1, 16]], ZC, 0)
        if not last:
            for p in range(t + 1):
                mm(a("p%d" % (3 + p // 2), NV * (p % 2), NV * (p % 2) + nv), [(a("r%d" % p), a("h16", 0, nv))])
        for (e, lo, hi) in cut(GA):
            chain("g" + e, lin(e, a("xq", 16 * lo + 16, 16 * hi + 16), ind(a("qw"), a("offq", lo, hi)), scale=2.0 ** -5))
        for ci, (b0, b1) in enumerate(cut(POST)):
            bank = "p%d" % ci
            for pi_, (lo, hi) in enumerate(cut(PRE)):
                if not b0 <= lo < b1:
                    continue
                pb = a(bank, lo - b0, hi - b0)
                x0, x1 = 16 * lo + 16, 16 * hi + 16
                chain("sum", mm(pb, [(a("i2b"), a("xq", x0 + k, x1, 16)) for k in range(16)]))
                iota(a("xq", x0 + 15, x1, 16), [[0, hi - lo]], NO, 0)
                tt(a("nt", lo, hi), pb, a("ub", uo + lo, uo + hi), A.mult)
                tt(a("w1", O + lo, O + hi), pb, a(wv, lo, hi), A.mult, extra=[arr_w] if hi > L else [])
                if ENG["d0"][pi_] == "v":
                    ts(a("ti", lo, hi), a("nt", lo, hi), 2047.0 + 255.0 / 512.0, None, A.add)
                    ts(a("d0", x0 - 1, x1 - 1, 16), a("ti", lo, hi), 2.0 ** -5, None, A.mult)
                else:
                    ts(a("nt", lo, hi), a("nt", lo, hi), 2047.0 + 255.0 / 512.0, 1.5 * 2 ** 23, A.add, A.add)
                    act(a("d0", x0 - 1, x1 - 1, 16), a("nt", lo, hi), scale=2.0 ** -5, bias=-1.5 * 2 ** 18)
                chain("scan", scan(a("dd", x0 - 1, x1 - 1), a("d0", x0 - 1, x1 - 1), a("xq", x0 - 1, x1 - 1), 60000.0, A.min, A.add))
                mm(a(bank, 128 + lo - b0, 128 + hi - b0), [(EB(k), a("dd", x0 + k, x1 - 1, 16)) for k in range(15)])
            lo, hi = b0, b1
            n = hi - lo
            pb = a(bank, 0, n)
            act(a("ge", lo, hi), a(bank, 128, 128 + n), AF.Sign, bias=c(THR))
            mm(pb, [(a("bid"), a("ge", lo, hi))])
            yy = a("yy", lo, hi)
            tt(yy, pb, a("nk16", lo, hi), A.mult)
            if not last:
                mm(a(bank, 256, 256 + n), [(a("b16"), yy)])
            hp = a(bank, 384, 384 + n) if last else a("p7", lo, hi)
            mm(hp, [(a("i16"), a("h16", lo, hi)), (E(t + 1), yy)])
            if last:
                act(a(hw, O + lo, O + hi), hp, bias=c(RB), scale=c(RM))
                continue
            act(a(hw, O + lo, O + hi), hp)
            scan(a("wsc", lo, hi), a("da", 0, n), a(bank, 256, 256 + n), 0.0, A.add, A.min)
            so = a("soff", 8 * ci, 8 * ci + n // 16)
            off(ENG["soff"][ci], so, a("wsc", lo + 15, hi, 16), c(AD))
            nk = a("nkn", lo, hi)
            lin(ENG["nkn"][ci], nk, ind(a("nbs"), so), bias=-1024.0)
            terms = [(a("i16"), nk)]
            for p in range(t + 2):
                hb = a(bank, 256, 256 + n) if p == t + 1 else a("p%d" % (3 + p // 2), NV * (p % 2) + lo, NV * (p % 2) + hi)
                tt(a("eqs", NV * p + lo, NV * p + hi), nk, hb, A.is_equal)
                terms.append((a("i4k"), a("eqs", NV * p + lo, NV * p + hi)))
            mm(a(bank, 128, 128 + n), terms)
            act(a("nkm", O + lo, O + hi), a(bank, 128, 128 + n))
        dst = a("srcw%d" % ((t + 1) % 2), 0, 1)
        if t > 0:
            cp(ind(a("w1", 0, NV), dst), a("w1", NV, NV + 16))
        w1 = a("w1", O, O + L)
        ts(a("mm", 0, L), w1, a(lh, 8 + t, 9 + t), None, A.is_gt)
        tt(a("mm", 224, 224 + L), w1, a("p5", 0, L), A.is_lt)
        ts(a("mm", 448, 640), w1, a(lh, t, t + 1), None, A.is_lt)
        mm(a("p5", 304, 496), [(a("b16"), a("mm", 0, L))])
        mm(a("p5", 0, L), [(a("b16"), a("mm", 224, 224 + L))])
        if ENG["fh"] == "s":
            act(a("fh", 0, L), a("p5", 304, 496), AF.Sign, bias=-9.5)
        else:
            ts(a("fh", 0, L), a("p5", 304, 496), 9.5, 2.0, A.is_gt, A.mult)
        act(a("junk", 0, L), a("p5", 0, L), AF.Sign, bias=-9.5, accum=s(NH))
        scan(a("rc"), a("fh"), a("big"), c(R0), A.add, A.add)
        act(a("junk"), a("rc"), AF.Sign, bias=s(NH), scale=-1.0, accum=s(NC))
        sur = a("sur", 2 * t, 2 * t + 1)
        lin(ENG["sur"], sur, s(NC), 0.5, float(NV // 2 + O))
        mm(a("p6", 0, 40), [(E(r), a("mm", r, 640, 16)) for r in range(16)])
        ts(a("fl", 1, 41), a("p6", 0, 40), 9.5, None, A.is_gt)
        one = a("one", p=1)
        mm(a("p6", 64, 92), [(one, a("kc", 0, 28, p=1)), (a("tri"), a("fl", 1, 29)), (a("upp"), a("fl", 0, 28))])
        scan(a("rr", 0, 28), a("d0c", 0, 28), a("p6", 64, 92), 0.0, A.mult, A.add)
        mm(a("p6", 92, 104), [(a("i16"), a("fl", 29, 41)), (a("i16"), a("fl", 15, 27)), (a("i2h"), a("fl", 1, 13))])
        off(ENG["cls"], a("lst", 28, 40), a("p6", 92, 104), float(MU))
        tt(a("lst", 0, 26), a("rr", 0, 26), a("idw"), A.max)
        tt(a("lst", 0, 12), a("lst", 0, 12), a("rr", 14, 26), A.max)
        if ENG["tb"] == "s":
            act(ind(a("tb", SW, TW), a("lst", 0, 12)), a("tb", 0, L), AF.Silu)
        else:
            cp(ind(a("tb", SW, TW), a("lst", 0, 12)), a("tb", 0, L))
        act(a("srcb"), ind(a("tb"), a("lst", 12, 26)))
        act(a("mu"), ind(a("tb", 0, SW), a("lst", 28, 40)))
        if t > 0:
            if not last:
                cp(ind(a("nkm", 0, NV), dst), a("nkm", NV, NV + 16))
            cp(ind(a(hw, 0, NV), dst), a(hw, NV, NV + 16))
        scan(a("ssc"), a("ds", 0, 224), a("srcb"), 0.0, A.add, A.min)
        sw = "srcw%d" % (t % 2)
        off(ENG["srcw"], a(sw, 0, 14), a("ssc", 15, 224, 16), c(AD2))
        dst = a(sw, 0, 1); src = a(sw, 2, 14)
        so_ = 32 * t; wn = "wv%d" % (t + 1)
        if not last:
            for (e, lo, hi) in OFFQ:
                off(e, a("offq", lo, hi), ind(a("nkm"), a(sw, 2 + lo // 16, 2 + hi // 16)), 1040.0)
        act(a("snd", so_, so_ + 16), ind(a("w1"), sur), scale=0.5)
        act(a("snd", so_ + 16, so_ + 32), ind(a(hw), sur))
        rid, pid, _ = topo.addr(nxt)
        msk = topo.mask(core, nxt)
        ne = len(topo.engines(core, nxt))

        def send(so_=so_, wn=wn, t=t, rid=rid, pid=pid, msk=msk):
            g.remote_dma(T[wn][:, L:224], T.snd[:, so_:so_ + 32], T.sem["aw%d" % t], T.sem.loc, pid, rid, msk)
        sn = node("g", send, [], [a("snd", so_, so_ + 32)], {"fx": 0.3}, kind="r")
        nloc[0] += ne
        arr_w = node("x", None, [], [], {}, extra=[sn], lat="link", kind="a", sem="aw%d" % t, cnt=ne)
        if last:
            tt(a("wo", O, NV), ind(a("w1"), src), a("mu"), A.mult)
            act(a("ho", O, NV), ind(a(hw), src))
            cp(ind(a("wo"), dst), a(wn, L, NV), extra=[arr_w])
            cp(ind(a("ho"), dst), a(wn, NV, 224), extra=[arr_w])
            dma("y", rot_out(T.yw, "wo", O, NV), [], [a("wo")], 2.0)
            dma("s", rot_out(T.yh, "ho", O, NV), [], [a("ho")], 2.0)
        else:
            tt(a(wn, 0, L), ind(a("w1"), src), a("mu"), A.mult)
            lin(ENG["h16"], a("h16", 0, L), ind(a(hw), src))
            uo2 = uo + NV
            act(a("ub", uo2 + L, uo2 + NV), ind(a("ub", uo2 - O, uo2 + L), dst))
            act(s(YY), a("rc", NV - 1, NV), bias=s(NH), scale=-1.0)
            dif = a("dif", 8 * t, 8 * t + 1)
            ts(dif, s(PD), c(ID), s(YY), A.max, A.subtract)
            m7 = msk
            for q in peers:
                m7 = m7 & topo.mask(core, q)
            n7 = bin(m7).count("1")

            def sendf(dif=dif, t=t, m7=m7):
                ids = [DstId(rid=topo.addr(q)[0], pnc=topo.addr(q)[1]) for q in peers]
                tr = RemoteDMATransfer(dst_ids=ids, dma_engine_mask=m7, remote_sem=T.sem["af%d" % t], srcs=[dif["ap"]],
                                       dsts=[T.cnt[:, 8 * t + rank:8 * t + rank + 1] for q in peers])
                g.remote_dma_fused([tr], local_sem=T.sem.loc)
            sf = node("g", sendf, [], [dif], {"fx": 0.5}, kind="r")
            nodes[sf]["after"].append(sn)
            nloc[0] += n7
            arr_f = node("x", None, [], [], {}, extra=[sf], lat="dif", kind="a", sem="af%d" % t, cnt=n7 * (n_r - 1))
    return nodes, nloc[0]


def schedule(nodes):
    n = len(nodes)
    anc = [0] * n
    pred = []
    for k in range(n):
        deps = nodes[k]["deps"] + nodes[k]["after"]
        cover = 0
        for d in deps:
            cover |= anc[d]
        pred.append(sorted(set(d for d in deps if not cover >> d & 1)))
        for d in pred[k]:
            cover |= 1 << d
        anc[k] = cover
    cost = [price(x, COST) for x in nodes]; eng = [x["e"] for x in nodes]
    lag = [COST.get(x["lat"], x["lat"] or 0.0) + COST["hop"] for x in nodes]
    arc = [[(d, lag[d] if d in nodes[k]["deps"] else 0.0) for d in pred[k]] for k in range(n)]
    rev = [[] for _ in range(n)]
    for k in range(n):
        for d, w in arc[k]:
            rev[d].append((k, w))
    back = range(n - 1, -1, -1)
    ends = [k for k in range(n) if not rev[k]]
    marks = [k for k in range(n) if nodes[k]["k"] == "a"]

    def run(order, arcs):
        busy = {e: ([], [], []) for e in set(eng)}
        st = [0.0] * n; fin = [0.0] * n; why = [-1] * n
        for k in order:
            t0 = lag[k] if arcs is rev and not arcs[k] else 0.0
            y = -1
            for j, w in arcs[k]:
                if fin[j] + w > t0:
                    t0 = fin[j] + w; y = j
            d = cost[k]
            if d > 0:
                bs, be, bk = busy[eng[k]]
                i = m = len(bs)
                while i > 0 and be[i - 1] > t0:
                    i -= 1
                while i < m and t0 + d > bs[i] + 1e-9:
                    if be[i] > t0:
                        t0 = be[i]; y = -2 - bk[i]
                    i += 1
                bs.insert(i, t0); be.insert(i, t0 + d); bk.insert(i, k)
            st[k] = t0; fin[k] = t0 + d; why[k] = y
        return st, fin, why

    def legal(key, turn=False):
        key = list(key)
        nxt = arc if turn else rev
        for k in (range(n) if turn else back):
            for j, _ in nxt[k]:
                if key[k] >= key[j]:
                    key[k] = key[j] - 1e-6
        return sorted(range(n), key=lambda z: key[z])

    def fore(key):
        st, fin, why = run(legal(key), arc)
        k = max(ends, key=lambda z: fin[z] + lag[z])
        end = fin[k] + lag[k]
        pairs = []
        while why[k] != -1:
            if why[k] <= -2:
                pairs.append((-2 - why[k], k)); k = -2 - why[k]
            else:
                k = why[k]
        return (end + MARK * sum(fin[z] for z in marks) + 1e-5 * sum(fin), st, end, pairs, fin)

    def turn(c):
        return fore([-z for z in run(legal([-z for z in c[4]], True), rev)[1]])
    seed = [SEED]

    def rnd():
        seed[0] = (seed[0] * 1103515245 + 12345) % 2147483648
        return seed[0] / 2147483648.0
    bl = [0.0] * n
    for k in back:
        bl[k] = cost[k] + max([bl[j] + w for j, w in rev[k]], default=lag[k])
    cur = best = turn(turn(fore([-x for x in bl])))
    for it in range(ROUNDS):
        key = list(cur[1])
        for _ in range(1 + int(rnd() * 2)):
            r = rnd()
            if r < 0.7 and cur[3]:
                u, v = cur[3][int(rnd() * len(cur[3]))]
                d = key[v] - key[u] + 1e-3 + rnd() * rnd() * 1.5
                if r < 0.35:
                    u, d = v, -d
            else:
                u = int(rnd() * n); d = (rnd() - 0.5) * 3.0 * rnd()
            key[u] += d
            ks = [u]
            while d > 0 and ks:
                nx = []
                for z in ks:
                    for j, _w in rev[z]:
                        if key[j] <= key[z]:
                            key[j] = key[z] + 1e-6; nx.append(j)
                ks = nx
        c2 = fore(key)
        if rnd() < TURN:
            c2 = min(c2, turn(c2), key=lambda z: z[0])
        if c2[0] < cur[0] + TEMP * (1.0 - it / ROUNDS) * rnd():
            cur = c2
            if c2[0] < best[0]:
                best = c2
    return legal(best[1]), best[1], best[2]


ORDER = []


def rank_program(g, core, T, topo):
    if T.rank_of(core) is None:
        return
    nodes, nloc = build(g, core, T, topo)
    if not ORDER:
        ORDER.append(schedule(nodes)[0])
    order = ORDER[0]
    q = {"v": g.vector, "s": g.scalar, "t": g.tensor, "g": g, "y": g.sync}
    count = {"v": 0, "s": 0, "t": 0, "g": 0}
    clock = {e: {} for e in q}
    done = {}
    last = {}
    for k in order:
        x = nodes[k]
        if x["k"] == "a":
            done[k] = (x["sem"], x["cnt"], {})
            last[x["sem"]] = x["cnt"]
            continue
        e = x["e"]; ck = clock[e]
        need = [done[d] for d in x["deps"] if done[d] is not None]
        need.sort(key=lambda z: -z[1])
        for (sem, cnt, c2) in need:
            if ck.get(sem, 0) < cnt and not any(z[2].get(sem, 0) >= cnt for z in need):
                q[e].wait_ge(T.sem[sem], cnt)
            ck[sem] = max(ck.get(sem, 0), cnt)
            for s2, v2 in c2.items():
                if ck.get(s2, 0) < v2:
                    ck[s2] = v2
        r = x["f"]()
        if x["k"] == "c":
            count[e] += 1
            r.then_inc(T.sem["e" + e], 1)
            done[k] = ("e" + e, count[e], dict(ck))
            last["e" + e] = count[e]
        elif x["k"] == "d":
            done[k] = (x["sem"], x["cnt"], dict(ck))
            last[x["sem"]] = x["cnt"]
        else:
            done[k] = None
    last["loc"] = nloc
    for sem, cnt in last.items():
        g.wait_ge(T.sem[sem], cnt)
